import numpy as np
import ml_dtypes


def mxq(x, axis, fmt="e4m3"):
    dtype, down = {"e4m3": (ml_dtypes.float8_e4m3fn, 7), "e5m2": (ml_dtypes.float8_e5m2, 14)}[fmt]
    v = np.moveaxis(np.asarray(x, np.float32).astype(ml_dtypes.bfloat16).astype(np.float64), axis, -1)
    blocks = v.reshape(v.shape[:-1] + (-1, 32))
    amax = np.abs(blocks).max(-1, keepdims=True)
    byte = np.maximum(np.where(amax > 0, np.frexp(amax)[1] - 1 + 127, 0) - down, 1)
    scale = np.exp2(byte - 127.0)
    codes = (blocks / scale).astype(np.float32).astype(dtype).astype(np.float64)
    return np.moveaxis((codes * scale).reshape(v.shape), -1, axis)


WIDE = False


def mx_kscale(k):
    if not WIDE:
        return np.ones(k)
    levels = np.array([10, -10, 5, -5, 0])
    if k % 512:
        return np.exp2(np.random.permutation(np.resize(levels, k // 32))).repeat(32)
    a = np.empty((k // 512, 16))
    for p in range(k // 512):
        a[p, :8] = np.random.permutation(np.resize(levels, 8))
        for g in range(8):
            far = levels[np.abs(levels - a[p, g]) >= 10]
            a[p, g + 8] = far[np.random.randint(len(far))]
    return np.exp2(a.ravel()).repeat(32)


def f64(x):
    return np.asarray(x).astype(np.float64)


def striped(idx):
    return np.tile(idx.reshape(-1, 16).T, (8, 1)).astype(np.uint16)


def unstriped(offs):
    return offs[:16].T.reshape(-1).astype(np.int64)


def striped8(idx):
    return np.concatenate([x.reshape(-1, 16).T for x in idx]).astype(np.uint16)


def runs(offs, k):
    lists = np.stack([offs[16 * r : 16 * r + 16].T.reshape(-1) for r in range(8)]).astype(np.int64)
    return lists[np.arange(k) % 512 // 64]


def pack_weight(w):
    k, n = w.shape
    w = f64(np.asarray(w, np.float32).astype(ml_dtypes.bfloat16)).reshape(k // 32, 32, n)
    amax = np.abs(w).max(1)
    byte = np.clip(np.where(amax > 0, np.frexp(amax)[1] - 1 + 127 - 7, 1), 1, 254)
    scaled = (w * np.exp2(127.0 - byte)[:, None, :]).reshape(k, n).astype(np.float32)
    words = np.ascontiguousarray(scaled.reshape(k // 512, 128, 4, n).transpose(0, 1, 3, 2)).astype(ml_dtypes.float8_e4m3fn).view(np.uint8)
    return words, np.ascontiguousarray(byte.astype(np.uint8).reshape(k // 512, 16, n))


def unpack_weight(words, scales):
    g, p, n, _ = words.shape
    vals = np.ascontiguousarray(words).view(ml_dtypes.float8_e4m3fn).astype(np.float64) * np.repeat(np.exp2(scales.astype(np.float64) - 127.0), 8, axis=1)[..., None]
    return vals.transpose(0, 1, 3, 2).reshape(g * 512, n)


E2M1 = np.array([0.0, 0.5, 1.0, 1.5, 2.0, 3.0, 4.0, 6.0, -0.0, -0.5, -1.0, -1.5, -2.0, -3.0, -4.0, -6.0])


def pack_fp4(w):
    k, n = w.shape
    w = f64(np.asarray(w, np.float32).astype(ml_dtypes.bfloat16)).reshape(k // 32, 32, n)
    amax = np.abs(w).max(1)
    mant, ex = np.frexp(amax / 6.0)
    byte = np.clip(np.where(amax > 0, np.where(mant > 0.5, ex, ex - 1) + 127, 1), 1, 254)
    scaled = (w * np.exp2(127.0 - byte)[:, None, :]).reshape(k, n).astype(np.float32)
    c = np.ascontiguousarray(scaled.reshape(k // 512, 128, 4, n).transpose(0, 1, 3, 2)).astype(ml_dtypes.float4_e2m1fn).view(np.uint8) & 0xF
    words = (c[..., 0::2] | (c[..., 1::2] << 4)).reshape(k // 512, 128, 2 * n)
    return np.ascontiguousarray(words), np.ascontiguousarray(byte.astype(np.uint8).reshape(k // 512, 16, n))


def unpack_fp4(words, scales):
    g, _, n = scales.shape
    words = np.ascontiguousarray(words).reshape(g, 128, n, 2)
    nib = np.empty((g, 128, n, 4), np.uint8)
    nib[..., 0::2] = words & 0xF
    nib[..., 1::2] = words >> 4
    vals = E2M1[nib] * np.repeat(np.exp2(scales.astype(np.float64) - 127.0), 8, axis=1)[..., None]
    return vals.transpose(0, 1, 3, 2).reshape(g * 512, n)


def planes(y):
    n, m = y.shape
    v = y.astype(np.float32).astype(ml_dtypes.bfloat16).astype(np.float64).reshape(n // 32, 32, m)
    top = np.abs(v).max(1)
    byte = np.clip(np.where(top > 0, np.frexp(top)[1] - 1 + 127 - 7, 1), 1, 254)
    codes = (v * np.exp2(127.0 - byte)[:, None, :]).reshape(n, m).astype(np.float32).astype(ml_dtypes.float8_e4m3fn).view(np.uint8)
    words = codes.reshape(n // 512, 128, 4, m).transpose(0, 1, 3, 2)
    return np.ascontiguousarray(words), np.ascontiguousarray(byte.astype(np.uint8).reshape(n // 512, 16, m))


K, T, S, N, G, H = 512, 1024, 512, 512, 2048, 512


def setup_inputs():
    n = np.random.standard_normal
    s = mx_kscale(K)[:, None]
    u = mx_kscale(S)
    packed_xT = pack_weight(n((K, T)) * s)
    packed_dT = pack_weight(n((K, G)) / s)
    packed_w1 = pack_fp4(n((H, N)) / np.sqrt(H) / u[:, None])
    return {
        "x_words": packed_xT[0],
        "x_scales": packed_xT[1],
        "d_words": packed_dT[0],
        "d_scales": packed_dT[1],
        "gn": (np.random.uniform(0.5, 1.5, (H, 1)) * u[:, None]).astype(np.float32),
        "w1_words": packed_w1[0],
        "w1_scales": packed_w1[1],
        "offs": striped(np.random.permutation(T)[:S]),
        "k1": striped8(np.random.randint(0, G, (8, H))),
        "two": striped(np.random.permutation(T)[:S]),
        "k2": striped8(np.random.randint(0, G, (8, H))),
        "n1": striped8(np.stack([np.random.permutation(S) for _ in range(8)])),
        "n2": striped8(np.stack([np.random.permutation(S) for _ in range(8)])),
        "n3": striped8(np.stack([np.random.permutation(S) for _ in range(8)])),
    }


def reference(x_words, x_scales, d_words, d_scales, gn, w1_words, w1_scales, offs, k1, two, k2, n1, n2, n3):
    d_k1 = unpack_weight(d_words, d_scales)[np.arange(K)[:, None], runs(k1, K)]
    xq = unpack_weight(x_words, x_scales)[:, unstriped(offs)]
    a = 0.0625 * (d_k1.T @ xq)
    d_k2 = unpack_weight(d_words, d_scales)[np.arange(K)[:, None], runs(k2, K)]
    x_two = unpack_weight(x_words, x_scales)[:, unstriped(two)]
    b = 0.0625 * (d_k2.T @ x_two)
    z = f64(gn) * (0.75 * (a * (b[np.arange(H)[:, None], runs(n2, H)]) - ((a[np.arange(H)[:, None], runs(n1, H)]) * b)))
    h = unpack_fp4(w1_words, w1_scales).T @ mxq(z, 0, "e4m3")
    out_0 = h - (h[np.arange(N)[:, None], runs(n3, N)])
    return (out_0,) + planes(out_0)

@@ -1,0 +1,263 @@
+from contextlib import ExitStack
+
+import concourse.mybir as mybir
+
+F32 = mybir.dt.float32
+BF16 = mybir.dt.bfloat16
+I32 = mybir.dt.int32
+U32 = mybir.dt.uint32
+U16 = mybir.dt.uint16
+U8 = mybir.dt.uint8
+FP8X4 = mybir.dt.float8_e4m3fn_x4
+FP4X4 = mybir.dt.float4_e2m1fn_x4
+COPY = mybir.ActivationFunctionType.Copy
+MULT = mybir.AluOpType.mult
+ADD = mybir.AluOpType.add
+SUB = mybir.AluOpType.subtract
+
+P = 128
+PACK = 4
+S = 512
+TOKENS = 1024
+CODEWORDS = 2048
+HALF = S // 2
+LIST_COLS = S // 16
+FLOPS = 3 * 2 * 512 * 512 * 512
+
+
+def tile_picked_twpqcrossbdif_none_po_kernel(
+    tc, x_words, x_scales, d_words, d_scales, gn, w1_words, w1_scales, offs, k1, two, k2, n1, n2, n3,
+    out_0, out_1, out_2,
+):
+    nc = tc.nc
+    with ExitStack() as ctx:
+        keep = ctx.enter_context(tc.tile_pool(name="keep", bufs=1))
+        psum = ctx.enter_context(tc.psum_pool(name="psum", bufs=1))
+
+        def sb(name, shape, dtype, tag=None):
+            return keep.tile(shape, dtype, name=name, tag=tag or name, align_bytes=64)
+
+        def load_list(name, src):
+            tile = keep.tile([P, LIST_COLS], U16, name=name)
+            nc.sync.dma_start(tile[:], src)
+            return tile
+
+        def half_cols(h):
+            return slice(h * HALF, (h + 1) * HALF)
+
+        def half_list(tile, h):
+            return tile[:, h * (LIST_COLS // 2) : (h + 1) * (LIST_COLS // 2)]
+
+        d_scale_tab = sb("d_scale_tab", [P, CODEWORDS], U8)
+        x_scale_tab = sb("x_scale_tab", [P, TOKENS], U8)
+        offs_t = load_list("offs_t", offs)
+        nc.sync.dma_start(
+            x_scale_tab[:].bitcast(I32),
+            x_scales[0].bitcast(I32).unsqueeze(1).broadcast_to([16, 8, TOKENS // 4]),
+        )
+        k1_t = load_list("k1_t", k1)
+        nc.sync.dma_start(
+            d_scale_tab[:].bitcast(I32),
+            d_scales[0].bitcast(I32).unsqueeze(1).broadcast_to([16, 8, CODEWORDS // 4]),
+        )
+        x_tab = sb("x_tab", [P, TOKENS], U32)
+        d_tab = sb("d_tab", [P, CODEWORDS], U32)
+        nc.sync.dma_start(x_tab[:].bitcast(I32), x_words[0].rearrange("p c r -> p (c r)").bitcast(I32))
+        k2_t = load_list("k2_t", k2)
+        two_t = load_list("two_t", two)
+        nc.sync.dma_start(d_tab[:].bitcast(I32), d_words[0].rearrange("p c r -> p (c r)").bitcast(I32))
+        n1_t = load_list("n1_t", n1)
+        n2_t = load_list("n2_t", n2)
+        n3_t = load_list("n3_t", n3)
+
+        placed = [sb(f"placed{i}", [P, 2 * S], U8) for i in range(2)]
+        for tile in placed:
+            nc.vector.memset(tile[:].bitcast(I32), 0)
+        w_scale_raw = sb("w_scale_raw", [P, S], U8)
+        nc.vector.memset(w_scale_raw[:].bitcast(I32), 0)
+        gain_raw = sb("gain_raw", [P, PACK], F32)
+        nc.gpsimd.dma_start(gain_raw[:], gn.rearrange("(p t) o -> p (t o)", t=PACK))
+        w_raw = sb("w_raw", [P, 2 * S], U8)
+        nc.gpsimd.dma_start(w_raw[:].bitcast(I32), w1_words[0].bitcast(I32))
+        for q in range(4):
+            nc.gpsimd.dma_start(
+                w_scale_raw[:].bitcast(I32)[32 * q : 32 * q + 4, :], w1_scales[0].bitcast(I32)[4 * q : 4 * q + 4, :]
+            )
+        gain = sb("gain", [P, PACK], F32)
+        nc.gpsimd.tensor_scalar(gain[:], gain_raw[:], 0.75 * 0.0625 * 0.0625, 0.0, MULT, ADD)
+
+        def first_product(i, d_list, x_list):
+            picked_scales = sb(f"picked_scales{i}", [P, 2 * S], U8, tag="picked_scales")
+            nc.vector.tensor_copy(picked_scales[:, S:], x_scale_tab[:].indirect(x_list[:]))
+            nc.vector.tensor_copy(picked_scales[:, :S], d_scale_tab[:].indirect(d_list[:]))
+            for q in range(4):
+                nc.sync.dma_start(
+                    placed[i][:].bitcast(I32)[32 * q : 32 * q + 4, :],
+                    picked_scales[:].bitcast(I32)[32 * q : 32 * q + 32 : 8, :],
+                )
+            x_picked = sb(f"x_picked{i}", [P, S], U32, tag="x_picked")
+            d_picked = sb(f"d_picked{i}", [P, S], U32, tag=f"d_words{i}")
+            nc.vector.tensor_copy(x_picked[:], x_tab[:].indirect(x_list[:]))
+            nc.vector.tensor_copy(d_picked[:], d_tab[:].indirect(d_list[:]))
+            d_dealt = sb(f"d_dealt{i}", [P, S], U32, tag=f"d_words{i + 1}")
+            nc.vector.tensor_copy(
+                d_dealt[:].rearrange("p (t c i) -> p c t i", t=PACK, i=4),
+                d_picked[:].rearrange("p (c i t) -> p c t i", t=PACK, i=4),
+            )
+            d_scale_dealt = sb(f"d_scale_dealt{i}", [P, S], U8)
+            nc.vector.tensor_copy(
+                d_scale_dealt[:].rearrange("p (t c i) -> p c t i", t=PACK, i=16),
+                placed[i][:, :S].rearrange("p (c i t) -> p c t i", t=PACK, i=16),
+            )
+            banks = []
+            for t in range(PACK):
+                bank = psum.tile([P, S], F32, name=f"first{i}_{t}", tag=f"bank{PACK * i + t}")
+                cols = slice(t * P, (t + 1) * P)
+                nc.tensor.matmul_mx(
+                    out=bank[:],
+                    lhsT=d_dealt[:, cols].bitcast(FP8X4),
+                    lhsT_scale=d_scale_dealt[:, cols],
+                    rhs=x_picked[:].bitcast(FP8X4),
+                    rhs_scale=placed[i][:, S:],
+                    start=True,
+                    stop=True,
+                )
+                banks.append(bank)
+            return banks
+
+        a_banks = first_product(0, k1_t, offs_t)
+        a_rows = [sb(f"a_rows{t}", [P, S], F32) for t in range(PACK)]
+        a_at = [sb(f"a_at{t}", [P, S], F32) for t in range(PACK)]
+        for t in range(PACK):
+            nc.scalar.activation(a_rows[t][:], a_banks[t][:], COPY, scale=gain[:, t : t + 1])
+        for t in range(PACK):
+            for h in range(2):
+                nc.scalar.activation(a_at[t][:, half_cols(h)], a_rows[t][:].indirect(half_list(n1_t, h)), COPY)
+
+        b_banks = first_product(1, k2_t, two_t)
+
+        w_dealt = sb("w_dealt", [P, 2 * S], U8, tag="picked_scales")
+        nc.vector.tensor_copy(
+            w_dealt[:].rearrange("p (t c i b) -> p c t i b", t=PACK, i=8, b=2),
+            w_raw[:].rearrange("p (c i t b) -> p c t i b", t=PACK, i=8, b=2),
+        )
+        w_scale_dealt = sb("w_scale_dealt", [P, S], U8, tag="d_words1")
+        nc.vector.tensor_copy(
+            w_scale_dealt[:].rearrange("p (t c i) -> p c t i", t=PACK, i=16),
+            w_scale_raw[:].rearrange("p (c i t) -> p c t i", t=PACK, i=16),
+        )
+
+        b_rows = [sb(f"b_rows{t}", [P, S], F32) for t in range(PACK)]
+        second = sb("second", [P, PACK, S], F32)
+        for t in range(PACK):
+            nc.vector.tensor_tensor(second[:, t, :], b_banks[t][:], a_at[t][:], MULT)
+        for t in range(PACK):
+            nc.scalar.copy(b_rows[t][:], b_banks[t][:])
+
+        h_rows = [sb(f"h_rows{t}", [P, S], F32) for t in range(PACK)]
+        first = [sb(f"first{h}", [P, PACK, HALF], F32) for h in range(2)]
+        z_pairs = [sb(f"z_pairs{h}", [P, 2, HALF, 2], BF16) for h in range(2)]
+        z_grouped = [sb(f"z_grouped{h}", [P, HALF * PACK], BF16) for h in range(2)]
+        b_at = [[sb(f"b_at{h}_{t}", [P, HALF], F32) for t in range(PACK)] for h in range(2)]
+
+        def fetch_b(h, t):
+            looked_up = b_rows[t][:].indirect(half_list(n2_t, h))
+            if t < 1:
+                nc.vector.tensor_copy(b_at[h][t][:], looked_up)
+            else:
+                nc.scalar.activation(b_at[h][t][:], looked_up, COPY)
+
+        def first_term(h, t):
+            nc.vector.scalar_tensor_tensor(
+                first[h][:, t, :], a_banks[t][:, half_cols(h)], gain[:, t : t + 1], b_at[h][t][:], MULT, MULT
+            )
+
+        def subtract(h, u):
+            nc.vector.tensor_tensor(
+                z_pairs[h][:, u, :, :],
+                first[h][:, 2 * u : 2 * u + 2, :].rearrange("p t j -> p j t"),
+                second[:, 2 * u : 2 * u + 2, half_cols(h)].rearrange("p t j -> p j t"),
+                SUB,
+            )
+
+        def weave(h):
+            nc.vector.tensor_copy(
+                z_grouped[h][:].bitcast(I32).rearrange("p (j u) -> p j u", u=2),
+                z_pairs[h][:].rearrange("p u j e -> p (u j e)").bitcast(I32).rearrange("p (u j) -> p j u", u=2),
+            )
+
+        def last_product(h):
+            z_codes = sb(f"z_codes{h}", [P, HALF], U32)
+            z_scales = sb(f"z_scales{h}", [P, HALF], U8)
+            nc.vector.quantize_mx(out=z_codes[:].bitcast(FP8X4), scales=z_scales[:], in_=z_grouped[h][:])
+            banks = []
+            for t in range(PACK):
+                bank = psum.tile([P, S], F32, name=f"h{h}_{t}", tag=f"bank{PACK * (1 - h) + t}")
+                nc.tensor.matmul_mx(
+                    out=bank[:, :HALF],
+                    lhsT=w_dealt[:, t * 2 * P : (t + 1) * 2 * P].bitcast(FP4X4),
+                    lhsT_scale=w_scale_dealt[:, t * P : (t + 1) * P],
+                    rhs=z_codes[:].bitcast(FP8X4),
+                    rhs_scale=z_scales[:],
+                    start=True,
+                    stop=True,
+                )
+                banks.append(bank)
+            return banks
+
+        for t in range(1):
+            for h in range(2):
+                fetch_b(h, t)
+                first_term(h, t)
+        for h in range(2):
+            for t in range(1, PACK):
+                fetch_b(h, t)
+        first_term(0, 1)
+        first_term(0, 2)
+        subtract(0, 0)
+        first_term(0, 3)
+        subtract(0, 1)
+        first_term(1, 1)
+        weave(0)
+        subtract(1, 0)
+        h_banks = [last_product(0)]
+        first_term(1, 2)
+        first_term(1, 3)
+        subtract(1, 1)
+        weave(1)
+        h_banks.append(last_product(1))
+        for h in range(2):
+            for t in range(PACK):
+                if h == 1 and t % 2 == 0:
+                    nc.vector.tensor_copy(h_rows[t][:, half_cols(h)], h_banks[h][t][:, :HALF])
+                else:
+                    nc.scalar.copy(h_rows[t][:, half_cols(h)], h_banks[h][t][:, :HALF])
+
+        out_rows = out_0.rearrange("(p t) j -> p t j", t=PACK)
+        out_words = out_1[0].rearrange("p c r -> p (c r)").bitcast(I32)
+        out_scales = sb("out_scales", [P, S], U8)
+        for h in range(2):
+            cols = half_cols(h)
+            result = sb(f"result{h}", [P, PACK, HALF], F32)
+            for t in range(PACK):
+                h_at = sb(f"h_at{h}_{t}", [P, HALF], F32)
+                if t < 1:
+                    nc.vector.tensor_copy(h_at[:], h_rows[t][:].indirect(half_list(n3_t, h)))
+                else:
+                    nc.scalar.activation(h_at[:], h_rows[t][:].indirect(half_list(n3_t, h)), COPY)
+                nc.vector.tensor_tensor(result[:, t, :], h_rows[t][:, cols], h_at[:], SUB)
+                if t % 2 == 1:
+                    nc.sync.dma_start(out_rows[:, t - 1 : t + 1, cols], result[:, t - 1 : t + 1, :])
+            grouped = sb(f"grouped{h}", [P, HALF * PACK], BF16)
+            nc.vector.tensor_copy(
+                grouped[:].rearrange("p (c i t) -> p c t i", t=PACK, i=4),
+                result[:].rearrange("p t (c i) -> p c t i", i=4),
+            )
+            codes = sb(f"codes{h}", [P, HALF], U32)
+            nc.vector.quantize_mx(out=codes[:].bitcast(FP8X4), scales=out_scales[:, cols], in_=grouped[:])
+            nc.sync.dma_start(out_words[:, cols], codes[:].bitcast(I32))
+        for q in range(4):
+            queue = nc.sync if q % 2 == 0 else nc.scalar
+            queue.dma_start(
+                out_2[0].bitcast(I32)[4 * q : 4 * q + 4, :], out_scales[:].bitcast(I32)[32 * q : 32 * q + 4, :]
+            )

@@ -32,14 +32,30 @@ def tile_picked_twpqcrossbdif_none_po_kernel(
     nc = tc.nc
     with ExitStack() as ctx:
         keep = ctx.enter_context(tc.tile_pool(name="keep", bufs=1))
+        reused = ctx.enter_context(tc.tile_pool(name="reused", bufs=1))
         psum = ctx.enter_context(tc.psum_pool(name="psum", bufs=1))
 
         def sb(name, shape, dtype, tag=None):
             return keep.tile(shape, dtype, name=name, tag=tag or name, align_bytes=64)
 
+        def sb_at(name, shape, dtype, offset):
+            return reused.tile(shape, dtype, name=name, align_bytes=64, offset=offset)
+
         def load_list(name, src):
             tile = keep.tile([P, LIST_COLS], U16, name=name)
             nc.sync.dma_start(tile[:], src)
+            return tile
+
+        def load_scale_table(name, src, width):
+            tile = sb(name, [P, width], U8)
+            nc.sync.dma_start(
+                tile[:].bitcast(I32), src[0].bitcast(I32).unsqueeze(1).broadcast_to([16, 8, width // 4])
+            )
+            return tile
+
+        def load_word_table(name, src, width):
+            tile = sb(name, [P, width], U32)
+            nc.sync.dma_start(tile[:].bitcast(I32), src[0].rearrange("p c r -> p (c r)").bitcast(I32))
             return tile
 
         def half_cols(h):
@@ -48,33 +64,23 @@ def tile_picked_twpqcrossbdif_none_po_kernel(
         def half_list(tile, h):
             return tile[:, h * (LIST_COLS // 2) : (h + 1) * (LIST_COLS // 2)]
 
-        d_scale_tab = sb("d_scale_tab", [P, CODEWORDS], U8)
-        x_scale_tab = sb("x_scale_tab", [P, TOKENS], U8)
         offs_t = load_list("offs_t", offs)
-        nc.sync.dma_start(
-            x_scale_tab[:].bitcast(I32),
-            x_scales[0].bitcast(I32).unsqueeze(1).broadcast_to([16, 8, TOKENS // 4]),
-        )
+        x_scale_tab = load_scale_table("x_scale_tab", x_scales, TOKENS)
         k1_t = load_list("k1_t", k1)
-        nc.sync.dma_start(
-            d_scale_tab[:].bitcast(I32),
-            d_scales[0].bitcast(I32).unsqueeze(1).broadcast_to([16, 8, CODEWORDS // 4]),
-        )
-        x_tab = sb("x_tab", [P, TOKENS], U32)
-        d_tab = sb("d_tab", [P, CODEWORDS], U32)
-        nc.sync.dma_start(x_tab[:].bitcast(I32), x_words[0].rearrange("p c r -> p (c r)").bitcast(I32))
-        k2_t = load_list("k2_t", k2)
+        d_scale_tab = load_scale_table("d_scale_tab", d_scales, CODEWORDS)
         two_t = load_list("two_t", two)
-        nc.sync.dma_start(d_tab[:].bitcast(I32), d_words[0].rearrange("p c r -> p (c r)").bitcast(I32))
+        x_tab = load_word_table("x_tab", x_words, TOKENS)
+        k2_t = load_list("k2_t", k2)
+        d_tab = load_word_table("d_tab", d_words, CODEWORDS)
         n1_t = load_list("n1_t", n1)
         n2_t = load_list("n2_t", n2)
         n3_t = load_list("n3_t", n3)
 
-        placed = [sb(f"placed{i}", [P, 2 * S], U8) for i in range(2)]
-        for tile in placed:
-            nc.vector.memset(tile[:].bitcast(I32), 0)
+        placed_a = sb("placed_a", [P, 2 * S], U8)
+        placed_b = sb("placed_b", [P, 2 * S], U8)
         w_scale_raw = sb("w_scale_raw", [P, S], U8)
-        nc.vector.memset(w_scale_raw[:].bitcast(I32), 0)
+        for tile in (placed_a, placed_b, w_scale_raw):
+            nc.vector.memset(tile[:].bitcast(I32), 0)
         gain_raw = sb("gain_raw", [P, PACK], F32)
         nc.gpsimd.dma_start(gain_raw[:], gn.rearrange("(p t) o -> p (t o)", t=PACK))
         w_raw = sb("w_raw", [P, 2 * S], U8)
@@ -86,18 +92,21 @@ def tile_picked_twpqcrossbdif_none_po_kernel(
         gain = sb("gain", [P, PACK], F32)
         nc.gpsimd.tensor_scalar(gain[:], gain_raw[:], 0.75 * 0.0625 * 0.0625, 0.0, MULT, ADD)
 
-        def first_product(i, d_list, x_list):
-            picked_scales = sb(f"picked_scales{i}", [P, 2 * S], U8, tag="picked_scales")
-            nc.vector.tensor_copy(picked_scales[:, S:], x_scale_tab[:].indirect(x_list[:]))
-            nc.vector.tensor_copy(picked_scales[:, :S], d_scale_tab[:].indirect(d_list[:]))
+        def place_scale_rows(placed, picked):
             for q in range(4):
                 nc.sync.dma_start(
-                    placed[i][:].bitcast(I32)[32 * q : 32 * q + 4, :],
-                    picked_scales[:].bitcast(I32)[32 * q : 32 * q + 32 : 8, :],
+                    placed[:].bitcast(I32)[32 * q : 32 * q + 4, :],
+                    picked[:].bitcast(I32)[32 * q : 32 * q + 32 : 8, :],
                 )
-            x_picked = sb(f"x_picked{i}", [P, S], U32, tag="x_picked")
+
+        def deal_bytes(dealt, plain):
+            nc.vector.tensor_copy(
+                dealt.rearrange("p (t c i) -> p c t i", t=PACK, i=16),
+                plain.rearrange("p (c i t) -> p c t i", t=PACK, i=16),
+            )
+
+        def first_product(i, d_list, d_scale_placed, x_picked, x_scale_placed, order):
             d_picked = sb(f"d_picked{i}", [P, S], U32, tag=f"d_words{i}")
-            nc.vector.tensor_copy(x_picked[:], x_tab[:].indirect(x_list[:]))
             nc.vector.tensor_copy(d_picked[:], d_tab[:].indirect(d_list[:]))
             d_dealt = sb(f"d_dealt{i}", [P, S], U32, tag=f"d_words{i + 1}")
             nc.vector.tensor_copy(
@@ -105,157 +114,209 @@ def tile_picked_twpqcrossbdif_none_po_kernel(
                 d_picked[:].rearrange("p (c i t) -> p c t i", t=PACK, i=4),
             )
             d_scale_dealt = sb(f"d_scale_dealt{i}", [P, S], U8)
-            nc.vector.tensor_copy(
-                d_scale_dealt[:].rearrange("p (t c i) -> p c t i", t=PACK, i=16),
-                placed[i][:, :S].rearrange("p (c i t) -> p c t i", t=PACK, i=16),
-            )
-            banks = []
-            for t in range(PACK):
-                bank = psum.tile([P, S], F32, name=f"first{i}_{t}", tag=f"bank{PACK * i + t}")
+            deal_bytes(d_scale_dealt[:], d_scale_placed)
+            banks = {}
+            for t in order:
+                banks[t] = psum.tile([P, S], F32, name=f"first{i}_{t}", tag=f"bank{PACK * i + t}")
                 cols = slice(t * P, (t + 1) * P)
                 nc.tensor.matmul_mx(
-                    out=bank[:],
+                    out=banks[t][:],
                     lhsT=d_dealt[:, cols].bitcast(FP8X4),
                     lhsT_scale=d_scale_dealt[:, cols],
                     rhs=x_picked[:].bitcast(FP8X4),
-                    rhs_scale=placed[i][:, S:],
+                    rhs_scale=x_scale_placed,
                     start=True,
                     stop=True,
                 )
-                banks.append(bank)
             return banks
 
-        a_banks = first_product(0, k1_t, offs_t)
+        picked_a = sb_at("picked_a", [P, 2 * S], U8, 2048)
+        nc.vector.tensor_copy(picked_a[:, S : 2 * S], x_scale_tab[:].indirect(offs_t[:]))
+        nc.vector.tensor_copy(picked_a[:, :S], d_scale_tab[:].indirect(k1_t[:]))
+        place_scale_rows(placed_a, picked_a)
+        x_picked_a = sb("x_picked_a", [P, S], U32)
+        nc.vector.tensor_copy(x_picked_a[:], x_tab[:].indirect(offs_t[:]))
+        a_banks = first_product(0, k1_t, placed_a[:, :S], x_picked_a, placed_a[:, S : 2 * S], (0, 1, 2, 3))
+
         a_rows = [sb(f"a_rows{t}", [P, S], F32) for t in range(PACK)]
-        a_at = [sb(f"a_at{t}", [P, S], F32) for t in range(PACK)]
+        a_at = [sb(f"a_at{t}", [P, S], F32) for t in range(3)]
         for t in range(PACK):
             nc.scalar.activation(a_rows[t][:], a_banks[t][:], COPY, scale=gain[:, t : t + 1])
-        for t in range(PACK):
+        for t in range(3):
             for h in range(2):
                 nc.scalar.activation(a_at[t][:, half_cols(h)], a_rows[t][:].indirect(half_list(n1_t, h)), COPY)
 
-        b_banks = first_product(1, k2_t, two_t)
+        picked_b = sb_at("picked_b", [P, 2 * S], U8, 2560)
+        nc.vector.tensor_copy(picked_b[:, S:], x_scale_tab[:].indirect(two_t[:]))
+        nc.vector.tensor_copy(picked_b[:, :S], d_scale_tab[:].indirect(k2_t[:]))
+        place_scale_rows(placed_b, picked_b)
+        x_picked_b = sb_at("x_picked_b", [P, S], U32, 512)
+        nc.vector.tensor_copy(x_picked_b[:], x_tab[:].indirect(two_t[:]))
+        b_order = (0, 1, 3, 2)
+        b_banks = first_product(1, k2_t, placed_b[:, :S], x_picked_b, placed_b[:, S:], b_order)
 
-        w_dealt = sb("w_dealt", [P, 2 * S], U8, tag="picked_scales")
+        w_dealt = sb_at("w_dealt", [P, 2 * S], U8, 3072)
         nc.vector.tensor_copy(
             w_dealt[:].rearrange("p (t c i b) -> p c t i b", t=PACK, i=8, b=2),
             w_raw[:].rearrange("p (c i t b) -> p c t i b", t=PACK, i=8, b=2),
         )
-        w_scale_dealt = sb("w_scale_dealt", [P, S], U8, tag="d_words1")
-        nc.vector.tensor_copy(
-            w_scale_dealt[:].rearrange("p (t c i) -> p c t i", t=PACK, i=16),
-            w_scale_raw[:].rearrange("p (c i t) -> p c t i", t=PACK, i=16),
-        )
+        w_scale_dealt = sb_at("w_scale_dealt", [P, S], U8, 2560)
+        deal_bytes(w_scale_dealt[:], w_scale_raw[:])
 
         b_rows = [sb(f"b_rows{t}", [P, S], F32) for t in range(PACK)]
         second = sb("second", [P, PACK, S], F32)
-        for t in range(PACK):
+        for t in range(3):
             nc.vector.tensor_tensor(second[:, t, :], b_banks[t][:], a_at[t][:], MULT)
-        for t in range(PACK):
+        for t in (3, 0, 1, 2):
             nc.scalar.copy(b_rows[t][:], b_banks[t][:])
 
-        h_rows = [sb(f"h_rows{t}", [P, S], F32) for t in range(PACK)]
-        first = [sb(f"first{h}", [P, PACK, HALF], F32) for h in range(2)]
+        first = sb("first", [P, PACK, S], F32)
+        b_at = [sb(f"b_at{t}", [P, S], F32) for t in range(PACK)]
         z_pairs = [sb(f"z_pairs{h}", [P, 2, HALF, 2], BF16) for h in range(2)]
         z_grouped = [sb(f"z_grouped{h}", [P, HALF * PACK], BF16) for h in range(2)]
-        b_at = [[sb(f"b_at{h}_{t}", [P, HALF], F32) for t in range(PACK)] for h in range(2)]
+        z_codes = [sb(f"z_codes{h}", [P, HALF], U32) for h in range(2)]
+        z_scales = [sb(f"z_scales{h}", [P, HALF], U8) for h in range(2)]
 
-        def fetch_b(h, t):
-            looked_up = b_rows[t][:].indirect(half_list(n2_t, h))
-            if t < 1:
-                nc.vector.tensor_copy(b_at[h][t][:], looked_up)
-            else:
-                nc.scalar.activation(b_at[h][t][:], looked_up, COPY)
+        def fetch_b(t, h):
+            nc.scalar.activation(b_at[t][:, half_cols(h)], b_rows[t][:].indirect(half_list(n2_t, h)), COPY)
 
-        def first_term(h, t):
+        def first_term(t, cols):
             nc.vector.scalar_tensor_tensor(
-                first[h][:, t, :], a_banks[t][:, half_cols(h)], gain[:, t : t + 1], b_at[h][t][:], MULT, MULT
+                first[:, t, cols], a_banks[t][:, cols], gain[:, t : t + 1], b_at[t][:, cols], MULT, MULT
             )
 
-        def subtract(h, u):
-            nc.vector.tensor_tensor(
+        def subtract(engine, u, h):
+            engine.tensor_tensor(
                 z_pairs[h][:, u, :, :],
-                first[h][:, 2 * u : 2 * u + 2, :].rearrange("p t j -> p j t"),
+                first[:, 2 * u : 2 * u + 2, half_cols(h)].rearrange("p t j -> p j t"),
                 second[:, 2 * u : 2 * u + 2, half_cols(h)].rearrange("p t j -> p j t"),
                 SUB,
             )
 
-        def weave(h):
-            nc.vector.tensor_copy(
-                z_grouped[h][:].bitcast(I32).rearrange("p (j u) -> p j u", u=2),
-                z_pairs[h][:].rearrange("p u j e -> p (u j e)").bitcast(I32).rearrange("p (u j) -> p j u", u=2),
+        def second_fused(t, h):
+            nc.vector.tensor_tensor(
+                second[:, t, half_cols(h)], a_rows[t][:].indirect(half_list(n1_t, h)), b_rows[t][:, half_cols(h)], MULT
             )
+
+        def first_fused(t, h):
+            nc.vector.tensor_tensor(
+                first[:, t, half_cols(h)], b_rows[t][:].indirect(half_list(n2_t, h)), a_rows[t][:, half_cols(h)], MULT
+            )
+
+        def weave(copy, h):
+            copy(
+                z_grouped[h][:].bitcast(U32).rearrange("p (j u) -> p j u", u=2),
+                z_pairs[h][:].rearrange("p u j e -> p (u j e)").bitcast(U32).rearrange("p (u j) -> p j u", u=2),
+            )
+
+        h_banks = [[None, None], [None, None]]
 
         def last_product(h):
-            z_codes = sb(f"z_codes{h}", [P, HALF], U32)
-            z_scales = sb(f"z_scales{h}", [P, HALF], U8)
-            nc.vector.quantize_mx(out=z_codes[:].bitcast(FP8X4), scales=z_scales[:], in_=z_grouped[h][:])
-            banks = []
-            for t in range(PACK):
-                bank = psum.tile([P, S], F32, name=f"h{h}_{t}", tag=f"bank{PACK * (1 - h) + t}")
-                nc.tensor.matmul_mx(
-                    out=bank[:, :HALF],
-                    lhsT=w_dealt[:, t * 2 * P : (t + 1) * 2 * P].bitcast(FP4X4),
-                    lhsT_scale=w_scale_dealt[:, t * P : (t + 1) * P],
-                    rhs=z_codes[:].bitcast(FP8X4),
-                    rhs_scale=z_scales[:],
-                    start=True,
-                    stop=True,
-                )
-                banks.append(bank)
-            return banks
+            nc.vector.quantize_mx(out=z_codes[h][:].bitcast(FP8X4), scales=z_scales[h][:], in_=z_grouped[h][:])
+            for u in range(2):
+                h_banks[h][u] = psum.tile([P, 2, HALF], F32, name=f"h{h}_{u}", tag=f"bank{PACK + 2 * h + u}")
+                for e in range(2):
+                    t = 2 * u + e
+                    nc.tensor.matmul_mx(
+                        out=h_banks[h][u][:, e, :],
+                        lhsT=w_dealt[:, t * 2 * P : (t + 1) * 2 * P].bitcast(FP4X4),
+                        lhsT_scale=w_scale_dealt[:, t * P : (t + 1) * P],
+                        rhs=z_codes[h][:].bitcast(FP8X4),
+                        rhs_scale=z_scales[h][:],
+                        start=True,
+                        stop=True,
+                    )
 
-        for t in range(1):
-            for h in range(2):
-                fetch_b(h, t)
-                first_term(h, t)
-        for h in range(2):
-            for t in range(1, PACK):
-                fetch_b(h, t)
-        first_term(0, 1)
-        first_term(0, 2)
-        subtract(0, 0)
-        first_term(0, 3)
-        subtract(0, 1)
-        first_term(1, 1)
-        weave(0)
-        subtract(1, 0)
-        h_banks = [last_product(0)]
-        first_term(1, 2)
-        first_term(1, 3)
-        subtract(1, 1)
-        weave(1)
-        h_banks.append(last_product(1))
-        for h in range(2):
-            for t in range(PACK):
-                if h == 1 and t % 2 == 0:
-                    nc.vector.tensor_copy(h_rows[t][:, half_cols(h)], h_banks[h][t][:, :HALF])
-                else:
-                    nc.scalar.copy(h_rows[t][:, half_cols(h)], h_banks[h][t][:, :HALF])
+        second_fused(3, 0)
+        second_fused(3, 1)
+        first_fused(0, 0)
+        for t in range(1, PACK):
+            fetch_b(t, 0)
+        first_term(1, half_cols(0))
+        first_fused(0, 1)
+        subtract(nc.vector, 0, 0)
+        first_term(2, half_cols(0))
+        first_term(3, half_cols(0))
+        fetch_b(1, 1)
+        fetch_b(2, 1)
+        subtract(nc.vector, 1, 0)
+        first_term(1, half_cols(1))
+        fetch_b(3, 1)
+        weave(nc.scalar.copy, 0)
+        first_term(2, half_cols(1))
+        subtract(nc.vector, 0, 1)
+        first_term(3, half_cols(1))
+        last_product(0)
+        subtract(nc.vector, 1, 1)
+        weave(nc.vector.tensor_copy, 1)
+        last_product(1)
 
+        h_rows = [sb(f"h_rows{t}", [P, S], F32) for t in range(PACK)]
+        h_at = [sb(f"h_at{h}", [P, PACK, HALF], F32) for h in range(2)]
+        result = [sb(f"result{h}", [P, PACK, HALF], F32) for h in range(2)]
+        grouped = [sb(f"grouped{h}", [P, HALF * PACK], BF16) for h in range(2)]
+        codes = [sb(f"codes{h}", [P, HALF], U32) for h in range(2)]
+        out_scales = sb("out_scales", [P, S], U8)
         out_rows = out_0.rearrange("(p t) j -> p t j", t=PACK)
         out_words = out_1[0].rearrange("p c r -> p (c r)").bitcast(I32)
-        out_scales = sb("out_scales", [P, S], U8)
-        for h in range(2):
-            cols = half_cols(h)
-            result = sb(f"result{h}", [P, PACK, HALF], F32)
-            for t in range(PACK):
-                h_at = sb(f"h_at{h}_{t}", [P, HALF], F32)
-                if t < 1:
-                    nc.vector.tensor_copy(h_at[:], h_rows[t][:].indirect(half_list(n3_t, h)))
-                else:
-                    nc.scalar.activation(h_at[:], h_rows[t][:].indirect(half_list(n3_t, h)), COPY)
-                nc.vector.tensor_tensor(result[:, t, :], h_rows[t][:, cols], h_at[:], SUB)
-                if t % 2 == 1:
-                    nc.sync.dma_start(out_rows[:, t - 1 : t + 1, cols], result[:, t - 1 : t + 1, :])
-            grouped = sb(f"grouped{h}", [P, HALF * PACK], BF16)
-            nc.vector.tensor_copy(
-                grouped[:].rearrange("p (c i t) -> p c t i", t=PACK, i=4),
-                result[:].rearrange("p t (c i) -> p c t i", i=4),
+
+        def copy_h(copy, t, h):
+            copy(h_rows[t][:, half_cols(h)], h_banks[h][t // 2][:, t % 2, :])
+
+        def fetch_h(t, h):
+            looked_up = h_rows[t][:].indirect(half_list(n3_t, h))
+            if (t, h) in ((2, 0), (3, 0)):
+                nc.vector.tensor_copy(h_at[h][:, t, :], looked_up)
+            else:
+                nc.scalar.activation(h_at[h][:, t, :], looked_up, COPY)
+
+        def store_pair(u, h):
+            pair = slice(2 * u, 2 * u + 2)
+            nc.sync.dma_start(out_rows[:, pair, half_cols(h)], result[h][:, pair, :])
+
+        def difference(u, h):
+            pair = slice(2 * u, 2 * u + 2)
+            nc.vector.tensor_tensor(result[h][:, pair, :], h_banks[h][u][:], h_at[h][:, pair, :], SUB)
+            store_pair(u, h)
+
+        def difference_one(engine, t, h):
+            source = h_banks[h][t // 2][:, t % 2, :] if engine is nc.vector else h_rows[t][:, half_cols(h)]
+            engine.tensor_tensor(result[h][:, t, :], source, h_at[h][:, t, :], SUB)
+
+        def group(copy, h):
+            copy(
+                grouped[h][:].rearrange("p (c i t) -> p c t i", t=PACK, i=4),
+                result[h][:].rearrange("p t (c i) -> p c t i", i=4),
             )
-            codes = sb(f"codes{h}", [P, HALF], U32)
-            nc.vector.quantize_mx(out=codes[:].bitcast(FP8X4), scales=out_scales[:, cols], in_=grouped[:])
-            nc.sync.dma_start(out_words[:, cols], codes[:].bitcast(I32))
+
+        def quantise(h):
+            nc.vector.quantize_mx(
+                out=codes[h][:].bitcast(FP8X4), scales=out_scales[:, half_cols(h)], in_=grouped[h][:]
+            )
+            nc.sync.dma_start(out_words[:, half_cols(h)], codes[h][:].bitcast(I32))
+
+        for t in range(PACK):
+            copy_h(nc.scalar.copy, t, 0)
+        copy_h(nc.scalar.copy, 0, 1)
+        copy_h(nc.scalar.copy, 1, 1)
+        copy_h(nc.vector.tensor_copy, 2, 1)
+        copy_h(nc.vector.tensor_copy, 3, 1)
+        fetch_h(0, 0)
+        fetch_h(1, 0)
+        fetch_h(2, 0)
+        fetch_h(3, 0)
+        difference(0, 0)
+        fetch_h(0, 1)
+        fetch_h(1, 1)
+        difference(1, 0)
+        fetch_h(2, 1)
+        fetch_h(3, 1)
+        group(nc.vector.tensor_copy, 0)
+        difference(0, 1)
+        quantise(0)
+        difference(1, 1)
+        group(nc.vector.tensor_copy, 1)
+        quantise(1)
         for q in range(4):
             queue = nc.sync if q % 2 == 0 else nc.scalar
             queue.dma_start(

@@ -12,7 +12,6 @@ FP8X4 = mybir.dt.float8_e4m3fn_x4
 FP4X4 = mybir.dt.float4_e2m1fn_x4
 COPY = mybir.ActivationFunctionType.Copy
 MULT = mybir.AluOpType.mult
-ADD = mybir.AluOpType.add
 SUB = mybir.AluOpType.subtract
 
 P = 128
@@ -22,6 +21,7 @@ TOKENS = 1024
 CODEWORDS = 2048
 HALF = S // 2
 LIST_COLS = S // 16
+FACTOR = 0.75 * 0.0625 * 0.0625
 FLOPS = 3 * 2 * 512 * 512 * 512
 
 
@@ -46,9 +46,9 @@ def tile_picked_twpqcrossbdif_none_po_kernel(
             nc.sync.dma_start(tile[:], src)
             return tile
 
-        def load_scale_table(name, src, width):
+        def load_scale_table(queue, name, src, width):
             tile = sb(name, [P, width], U8)
-            nc.sync.dma_start(
+            queue.dma_start(
                 tile[:].bitcast(I32), src[0].bitcast(I32).unsqueeze(1).broadcast_to([16, 8, width // 4])
             )
             return tile
@@ -65,9 +65,9 @@ def tile_picked_twpqcrossbdif_none_po_kernel(
             return tile[:, h * (LIST_COLS // 2) : (h + 1) * (LIST_COLS // 2)]
 
         offs_t = load_list("offs_t", offs)
-        x_scale_tab = load_scale_table("x_scale_tab", x_scales, TOKENS)
+        x_scale_tab = load_scale_table(nc.scalar, "x_scale_tab", x_scales, TOKENS)
         k1_t = load_list("k1_t", k1)
-        d_scale_tab = load_scale_table("d_scale_tab", d_scales, CODEWORDS)
+        d_scale_tab = load_scale_table(nc.sync, "d_scale_tab", d_scales, CODEWORDS)
         two_t = load_list("two_t", two)
         x_tab = load_word_table("x_tab", x_words, TOKENS)
         k2_t = load_list("k2_t", k2)
@@ -78,19 +78,10 @@ def tile_picked_twpqcrossbdif_none_po_kernel(
 
         placed_a = sb("placed_a", [P, 2 * S], U8)
         placed_b = sb("placed_b", [P, 2 * S], U8)
-        w_scale_raw = sb("w_scale_raw", [P, S], U8)
-        for tile in (placed_a, placed_b, w_scale_raw):
+        for tile in (placed_a, placed_b):
             nc.vector.memset(tile[:].bitcast(I32), 0)
-        gain_raw = sb("gain_raw", [P, PACK], F32)
-        nc.gpsimd.dma_start(gain_raw[:], gn.rearrange("(p t) o -> p (t o)", t=PACK))
-        w_raw = sb("w_raw", [P, 2 * S], U8)
-        nc.gpsimd.dma_start(w_raw[:].bitcast(I32), w1_words[0].bitcast(I32))
-        for q in range(4):
-            nc.gpsimd.dma_start(
-                w_scale_raw[:].bitcast(I32)[32 * q : 32 * q + 4, :], w1_scales[0].bitcast(I32)[4 * q : 4 * q + 4, :]
-            )
         gain = sb("gain", [P, PACK], F32)
-        nc.gpsimd.tensor_scalar(gain[:], gain_raw[:], 0.75 * 0.0625 * 0.0625, 0.0, MULT, ADD)
+        nc.gpsimd.dma_start(gain[:], gn.rearrange("(p t) o -> p (t o)", t=PACK))
 
         def place_scale_rows(placed, picked):
             for q in range(4):
@@ -105,10 +96,9 @@ def tile_picked_twpqcrossbdif_none_po_kernel(
                 plain.rearrange("p (c i t) -> p c t i", t=PACK, i=16),
             )
 
-        def first_product(i, d_list, d_scale_placed, x_picked, x_scale_placed, order):
-            d_picked = sb(f"d_picked{i}", [P, S], U32, tag=f"d_words{i}")
+        def first_product(i, d_picked, d_list, d_scale_placed, x_picked, x_scale_placed, order):
             nc.vector.tensor_copy(d_picked[:], d_tab[:].indirect(d_list[:]))
-            d_dealt = sb(f"d_dealt{i}", [P, S], U32, tag=f"d_words{i + 1}")
+            d_dealt = sb(f"d_dealt{i}", [P, S], U32, tag=f"d_words{i}")
             nc.vector.tensor_copy(
                 d_dealt[:].rearrange("p (t c i) -> p c t i", t=PACK, i=4),
                 d_picked[:].rearrange("p (c i t) -> p c t i", t=PACK, i=4),
@@ -136,7 +126,17 @@ def tile_picked_twpqcrossbdif_none_po_kernel(
         place_scale_rows(placed_a, picked_a)
         x_picked_a = sb("x_picked_a", [P, S], U32)
         nc.vector.tensor_copy(x_picked_a[:], x_tab[:].indirect(offs_t[:]))
-        a_banks = first_product(0, k1_t, placed_a[:, :S], x_picked_a, placed_a[:, S : 2 * S], (0, 1, 2, 3))
+        d_picked_a = sb_at("d_picked_a", [P, S], U32, 4096)
+        a_banks = first_product(0, d_picked_a, k1_t, placed_a[:, :S], x_picked_a, placed_a[:, S : 2 * S], (0, 1, 2, 3))
+
+        w_raw = sb_at("w_raw", [P, 2 * S], U8, 4096)
+        nc.sync.dma_start(w_raw[:].bitcast(I32), w1_words[0].bitcast(I32))
+        w_scale_raw = sb_at("w_scale_raw", [P, S], U8, 5120)
+        for q in range(4):
+            nc.sync.dma_start(
+                w_scale_raw[:].bitcast(I32)[32 * q : 32 * q + 32, :],
+                w1_scales[0].bitcast(I32)[4 * q : 4 * q + 4, :].unsqueeze(0).broadcast_to([8, 4, S // 4]),
+            )
 
         a_rows = [sb(f"a_rows{t}", [P, S], F32) for t in range(PACK)]
         a_at = [sb(f"a_at{t}", [P, S], F32) for t in range(3)]
@@ -153,7 +153,8 @@ def tile_picked_twpqcrossbdif_none_po_kernel(
         x_picked_b = sb_at("x_picked_b", [P, S], U32, 512)
         nc.vector.tensor_copy(x_picked_b[:], x_tab[:].indirect(two_t[:]))
         b_order = (0, 1, 3, 2)
-        b_banks = first_product(1, k2_t, placed_b[:, :S], x_picked_b, placed_b[:, S:], b_order)
+        d_picked_b = sb("d_picked_b", [P, S], U32, tag="d_words0")
+        b_banks = first_product(1, d_picked_b, k2_t, placed_b[:, :S], x_picked_b, placed_b[:, S:], b_order)
 
         w_dealt = sb_at("w_dealt", [P, 2 * S], U8, 3072)
         nc.vector.tensor_copy(
@@ -166,9 +167,9 @@ def tile_picked_twpqcrossbdif_none_po_kernel(
         b_rows = [sb(f"b_rows{t}", [P, S], F32) for t in range(PACK)]
         second = sb("second", [P, PACK, S], F32)
         for t in range(3):
-            nc.vector.tensor_tensor(second[:, t, :], b_banks[t][:], a_at[t][:], MULT)
+            nc.vector.scalar_tensor_tensor(second[:, t, :], b_banks[t][:], FACTOR, a_at[t][:], MULT, MULT)
         for t in (3, 0, 1, 2):
-            nc.scalar.copy(b_rows[t][:], b_banks[t][:])
+            nc.scalar.activation(b_rows[t][:], b_banks[t][:], COPY, scale=FACTOR)
 
         first = sb("first", [P, PACK, S], F32)
         b_at = [sb(f"b_at{t}", [P, S], F32) for t in range(PACK)]
@@ -187,9 +188,9 @@ def tile_picked_twpqcrossbdif_none_po_kernel(
 
         def subtract(engine, u, h):
             engine.tensor_tensor(
-                z_pairs[h][:, u, :, :],
-                first[:, 2 * u : 2 * u + 2, half_cols(h)].rearrange("p t j -> p j t"),
-                second[:, 2 * u : 2 * u + 2, half_cols(h)].rearrange("p t j -> p j t"),
+                z_pairs[h][:, u, :, :].rearrange("p (c i) e -> p c e i", i=4),
+                first[:, 2 * u : 2 * u + 2, half_cols(h)].rearrange("p e (c i) -> p c e i", i=4),
+                second[:, 2 * u : 2 * u + 2, half_cols(h)].rearrange("p e (c i) -> p c e i", i=4),
                 SUB,
             )
 
@@ -205,8 +206,8 @@ def tile_picked_twpqcrossbdif_none_po_kernel(
 
         def weave(copy, h):
             copy(
-                z_grouped[h][:].bitcast(U32).rearrange("p (j u) -> p j u", u=2),
-                z_pairs[h][:].rearrange("p u j e -> p (u j e)").bitcast(U32).rearrange("p (u j) -> p j u", u=2),
+                z_grouped[h][:].bitcast(U32).rearrange("p (c i u) -> p c u i", u=2, i=4),
+                z_pairs[h][:].rearrange("p u j e -> p (u j e)").bitcast(U32).rearrange("p (u c i) -> p c u i", u=2, i=4),
             )
 
         h_banks = [[None, None], [None, None]]
@@ -279,9 +280,8 @@ def tile_picked_twpqcrossbdif_none_po_kernel(
             nc.vector.tensor_tensor(result[h][:, pair, :], h_banks[h][u][:], h_at[h][:, pair, :], SUB)
             store_pair(u, h)
 
-        def difference_one(engine, t, h):
-            source = h_banks[h][t // 2][:, t % 2, :] if engine is nc.vector else h_rows[t][:, half_cols(h)]
-            engine.tensor_tensor(result[h][:, t, :], source, h_at[h][:, t, :], SUB)
+        def difference_aside(t, h):
+            nc.gpsimd.tensor_tensor(result[h][:, t, :], h_rows[t][:, half_cols(h)], h_at[h][:, t, :], SUB)
 
         def group(copy, h):
             copy(
@@ -298,7 +298,7 @@ def tile_picked_twpqcrossbdif_none_po_kernel(
         for t in range(PACK):
             copy_h(nc.scalar.copy, t, 0)
         copy_h(nc.scalar.copy, 0, 1)
-        copy_h(nc.scalar.copy, 1, 1)
+        copy_h(nc.vector.tensor_copy, 1, 1)
         copy_h(nc.vector.tensor_copy, 2, 1)
         copy_h(nc.vector.tensor_copy, 3, 1)
         fetch_h(0, 0)

@@ -12,6 +12,7 @@ FP8X4 = mybir.dt.float8_e4m3fn_x4
 FP4X4 = mybir.dt.float4_e2m1fn_x4
 COPY = mybir.ActivationFunctionType.Copy
 MULT = mybir.AluOpType.mult
+ADD = mybir.AluOpType.add
 SUB = mybir.AluOpType.subtract
 
 P = 128
@@ -210,23 +211,30 @@ def tile_picked_twpqcrossbdif_none_po_kernel(
                 z_pairs[h][:].rearrange("p u j e -> p (u j e)").bitcast(U32).rearrange("p (u c i) -> p c u i", u=2, i=4),
             )
 
-        h_banks = [[None, None], [None, None]]
+        h_pair_banks = []
+        h_psum = [[], []]
 
         def last_product(h):
             nc.vector.quantize_mx(out=z_codes[h][:].bitcast(FP8X4), scales=z_scales[h][:], in_=z_grouped[h][:])
-            for u in range(2):
-                h_banks[h][u] = psum.tile([P, 2, HALF], F32, name=f"h{h}_{u}", tag=f"bank{PACK + 2 * h + u}")
-                for e in range(2):
-                    t = 2 * u + e
-                    nc.tensor.matmul_mx(
-                        out=h_banks[h][u][:, e, :],
-                        lhsT=w_dealt[:, t * 2 * P : (t + 1) * 2 * P].bitcast(FP4X4),
-                        lhsT_scale=w_scale_dealt[:, t * P : (t + 1) * P],
-                        rhs=z_codes[h][:].bitcast(FP8X4),
-                        rhs_scale=z_scales[h][:],
-                        start=True,
-                        stop=True,
-                    )
+            for t in range(PACK):
+                if h == 0:
+                    if t % 2 == 0:
+                        h_pair_banks.append(
+                            psum.tile([P, 2, HALF], F32, name=f"h0_{t}", tag=f"bank{PACK + t // 2}")
+                        )
+                    h_psum[h].append(h_pair_banks[t // 2][:, t % 2, :])
+                else:
+                    bank = psum.tile([P, HALF], F32, name=f"h1_{t}", tag=f"bank{(PACK + 2 + t) % (2 * PACK)}")
+                    h_psum[h].append(bank[:])
+                nc.tensor.matmul_mx(
+                    out=h_psum[h][t],
+                    lhsT=w_dealt[:, t * 2 * P : (t + 1) * 2 * P].bitcast(FP4X4),
+                    lhsT_scale=w_scale_dealt[:, t * P : (t + 1) * P],
+                    rhs=z_codes[h][:].bitcast(FP8X4),
+                    rhs_scale=z_scales[h][:],
+                    start=True,
+                    stop=True,
+                )
 
         second_fused(3, 0)
         second_fused(3, 1)
@@ -262,7 +270,7 @@ def tile_picked_twpqcrossbdif_none_po_kernel(
         out_words = out_1[0].rearrange("p c r -> p (c r)").bitcast(I32)
 
         def copy_h(copy, t, h):
-            copy(h_rows[t][:, half_cols(h)], h_banks[h][t // 2][:, t % 2, :])
+            copy(h_rows[t][:, half_cols(h)], h_psum[h][t])
 
         def fetch_h(t, h):
             looked_up = h_rows[t][:].indirect(half_list(n3_t, h))
@@ -277,11 +285,23 @@ def tile_picked_twpqcrossbdif_none_po_kernel(
 
         def difference(u, h):
             pair = slice(2 * u, 2 * u + 2)
-            nc.vector.tensor_tensor(result[h][:, pair, :], h_banks[h][u][:], h_at[h][:, pair, :], SUB)
+            nc.vector.tensor_tensor(result[h][:, pair, :], h_pair_banks[u][:], h_at[h][:, pair, :], SUB)
             store_pair(u, h)
 
-        def difference_aside(t, h):
-            nc.gpsimd.tensor_tensor(result[h][:, t, :], h_rows[t][:, half_cols(h)], h_at[h][:, t, :], SUB)
+        def difference_one(t, h):
+            nc.vector.tensor_tensor(result[h][:, t, :], h_psum[h][t], h_at[h][:, t, :], SUB)
+            if t % 2 == 1:
+                store_pair(t // 2, h)
+
+        def group_aside(h):
+            nc.gpsimd.tensor_scalar(
+                grouped[h][:].rearrange("p (j t) -> p j t", t=PACK),
+                result[h][:].rearrange("p t j -> p j t"),
+                1.0,
+                0.0,
+                MULT,
+                ADD,
+            )
 
         def group(copy, h):
             copy(
@@ -298,23 +318,17 @@ def tile_picked_twpqcrossbdif_none_po_kernel(
         for t in range(PACK):
             copy_h(nc.scalar.copy, t, 0)
         copy_h(nc.scalar.copy, 0, 1)
-        copy_h(nc.vector.tensor_copy, 1, 1)
-        copy_h(nc.vector.tensor_copy, 2, 1)
-        copy_h(nc.vector.tensor_copy, 3, 1)
-        fetch_h(0, 0)
-        fetch_h(1, 0)
-        fetch_h(2, 0)
-        fetch_h(3, 0)
+        for t in range(1, PACK):
+            copy_h(nc.vector.tensor_copy, t, 1)
+        for t in range(PACK):
+            fetch_h(t, 0)
         difference(0, 0)
-        fetch_h(0, 1)
-        fetch_h(1, 1)
         difference(1, 0)
-        fetch_h(2, 1)
-        fetch_h(3, 1)
-        group(nc.vector.tensor_copy, 0)
-        difference(0, 1)
+        group_aside(0)
+        for t in range(PACK):
+            fetch_h(t, 1)
+            difference_one(t, 1)
         quantise(0)
-        difference(1, 1)
         group(nc.vector.tensor_copy, 1)
         quantise(1)
         for q in range(4):

@@ -22,8 +22,24 @@ TOKENS = 1024
 CODEWORDS = 2048
 HALF = S // 2
 LIST_COLS = S // 16
+BLOCKS = 16
+BLOCK_PARTS = 8
+QUADRANT = 32
 FACTOR = 0.75 * 0.0625 * 0.0625
-FLOPS = 3 * 2 * 512 * 512 * 512
+FLOPS = 3 * 2 * S * S * S
+
+A_TILES_ON_SCALAR = 3
+B_TILES_ON_VECTOR = 1
+H_TILES_ON_SCALAR = 2
+
+AT_X_PICKED_B = 512
+AT_PICKED_A = 2048
+AT_PICKED_B = 2560
+AT_W_SCALE_DEALT = 2560
+AT_W_DEALT = 3072
+AT_D_PICKED_A = 4096
+AT_W_RAW = 4096
+AT_W_SCALE_RAW = 5120
 
 
 def tile_picked_twpqcrossbdif_none_po_kernel(
@@ -42,15 +58,25 @@ def tile_picked_twpqcrossbdif_none_po_kernel(
         def sb_at(name, shape, dtype, offset):
             return reused.tile(shape, dtype, name=name, align_bytes=64, offset=offset)
 
+        def half_cols(h):
+            return slice(h * HALF, (h + 1) * HALF)
+
+        def half_list(tile, h):
+            return tile[:, h * (LIST_COLS // 2) : (h + 1) * (LIST_COLS // 2)]
+
+        def quadrant_rows(q):
+            return slice(QUADRANT * q, QUADRANT * q + 4)
+
         def load_list(name, src):
             tile = keep.tile([P, LIST_COLS], U16, name=name)
             nc.sync.dma_start(tile[:], src)
             return tile
 
-        def load_scale_table(queue, name, src, width):
+        def load_scale_table(name, src, width):
             tile = sb(name, [P, width], U8)
-            queue.dma_start(
-                tile[:].bitcast(I32), src[0].bitcast(I32).unsqueeze(1).broadcast_to([16, 8, width // 4])
+            nc.scalar.dma_start(
+                tile[:].bitcast(I32),
+                src[0].bitcast(I32).unsqueeze(1).broadcast_to([BLOCKS, BLOCK_PARTS, width // 4]),
             )
             return tile
 
@@ -59,16 +85,10 @@ def tile_picked_twpqcrossbdif_none_po_kernel(
             nc.sync.dma_start(tile[:].bitcast(I32), src[0].rearrange("p c r -> p (c r)").bitcast(I32))
             return tile
 
-        def half_cols(h):
-            return slice(h * HALF, (h + 1) * HALF)
-
-        def half_list(tile, h):
-            return tile[:, h * (LIST_COLS // 2) : (h + 1) * (LIST_COLS // 2)]
-
         offs_t = load_list("offs_t", offs)
-        x_scale_tab = load_scale_table(nc.scalar, "x_scale_tab", x_scales, TOKENS)
+        x_scale_tab = load_scale_table("x_scale_tab", x_scales, TOKENS)
         k1_t = load_list("k1_t", k1)
-        d_scale_tab = load_scale_table(nc.sync, "d_scale_tab", d_scales, CODEWORDS)
+        d_scale_tab = load_scale_table("d_scale_tab", d_scales, CODEWORDS)
         two_t = load_list("two_t", two)
         x_tab = load_word_table("x_tab", x_words, TOKENS)
         k2_t = load_list("k2_t", k2)
@@ -84,11 +104,13 @@ def tile_picked_twpqcrossbdif_none_po_kernel(
         gain = sb("gain", [P, PACK], F32)
         nc.gpsimd.dma_start(gain[:], gn.rearrange("(p t) o -> p (t o)", t=PACK))
 
-        def place_scale_rows(placed, picked):
-            for q in range(4):
-                nc.sync.dma_start(
-                    placed[:].bitcast(I32)[32 * q : 32 * q + 4, :],
-                    picked[:].bitcast(I32)[32 * q : 32 * q + 32 : 8, :],
+        def pick_scales(queue, picked, placed, d_list, x_list):
+            nc.vector.tensor_copy(picked[:, S:], x_scale_tab[:].indirect(x_list[:]))
+            nc.vector.tensor_copy(picked[:, :S], d_scale_tab[:].indirect(d_list[:]))
+            for q in range(BLOCKS // 4):
+                queue.dma_start(
+                    placed[:].bitcast(I32)[quadrant_rows(q), :],
+                    picked[:].bitcast(I32)[QUADRANT * q : QUADRANT * (q + 1) : BLOCK_PARTS, :],
                 )
 
         def deal_bytes(dealt, plain):
@@ -97,131 +119,132 @@ def tile_picked_twpqcrossbdif_none_po_kernel(
                 plain.rearrange("p (c i t) -> p c t i", t=PACK, i=16),
             )
 
-        def first_product(i, d_picked, d_list, d_scale_placed, x_picked, x_scale_placed, order):
+        def first_product(name, first_bank, d_picked, d_dealt, d_list, x_picked, placed, order):
             nc.vector.tensor_copy(d_picked[:], d_tab[:].indirect(d_list[:]))
-            d_dealt = sb(f"d_dealt{i}", [P, S], U32, tag=f"d_words{i}")
             nc.vector.tensor_copy(
                 d_dealt[:].rearrange("p (t c i) -> p c t i", t=PACK, i=4),
                 d_picked[:].rearrange("p (c i t) -> p c t i", t=PACK, i=4),
             )
-            d_scale_dealt = sb(f"d_scale_dealt{i}", [P, S], U8)
-            deal_bytes(d_scale_dealt[:], d_scale_placed)
+            d_scale_dealt = sb(f"d_scale_dealt_{name}", [P, S], U8)
+            deal_bytes(d_scale_dealt[:], placed[:, :S])
             banks = {}
             for t in order:
-                banks[t] = psum.tile([P, S], F32, name=f"first{i}_{t}", tag=f"bank{PACK * i + t}")
+                banks[t] = psum.tile([P, S], F32, name=f"{name}{t}", tag=f"bank{first_bank + t}")
                 cols = slice(t * P, (t + 1) * P)
                 nc.tensor.matmul_mx(
                     out=banks[t][:],
                     lhsT=d_dealt[:, cols].bitcast(FP8X4),
                     lhsT_scale=d_scale_dealt[:, cols],
                     rhs=x_picked[:].bitcast(FP8X4),
-                    rhs_scale=x_scale_placed,
+                    rhs_scale=placed[:, S:],
                     start=True,
                     stop=True,
                 )
             return banks
 
-        picked_a = sb_at("picked_a", [P, 2 * S], U8, 2048)
-        nc.vector.tensor_copy(picked_a[:, S : 2 * S], x_scale_tab[:].indirect(offs_t[:]))
-        nc.vector.tensor_copy(picked_a[:, :S], d_scale_tab[:].indirect(k1_t[:]))
-        place_scale_rows(placed_a, picked_a)
+        picked_a = sb_at("picked_a", [P, 2 * S], U8, AT_PICKED_A)
+        pick_scales(nc.scalar, picked_a, placed_a, k1_t, offs_t)
         x_picked_a = sb("x_picked_a", [P, S], U32)
         nc.vector.tensor_copy(x_picked_a[:], x_tab[:].indirect(offs_t[:]))
-        d_picked_a = sb_at("d_picked_a", [P, S], U32, 4096)
-        a_banks = first_product(0, d_picked_a, k1_t, placed_a[:, :S], x_picked_a, placed_a[:, S : 2 * S], (0, 1, 2, 3))
+        d_picked_a = sb_at("d_picked_a", [P, S], U32, AT_D_PICKED_A)
+        d_dealt_a = sb("d_dealt_a", [P, S], U32, tag="a_dealt_then_b_picked")
+        a_banks = first_product("a", 0, d_picked_a, d_dealt_a, k1_t, x_picked_a, placed_a, range(PACK))
 
-        w_raw = sb_at("w_raw", [P, 2 * S], U8, 4096)
+        w_raw = sb_at("w_raw", [P, 2 * S], U8, AT_W_RAW)
         nc.sync.dma_start(w_raw[:].bitcast(I32), w1_words[0].bitcast(I32))
-        w_scale_raw = sb_at("w_scale_raw", [P, S], U8, 5120)
-        for q in range(4):
+        w_scale_raw = sb_at("w_scale_raw", [P, S], U8, AT_W_SCALE_RAW)
+        for q in range(BLOCKS // 4):
             nc.sync.dma_start(
-                w_scale_raw[:].bitcast(I32)[32 * q : 32 * q + 32, :],
-                w1_scales[0].bitcast(I32)[4 * q : 4 * q + 4, :].unsqueeze(0).broadcast_to([8, 4, S // 4]),
+                w_scale_raw[:].bitcast(I32)[QUADRANT * q : QUADRANT * (q + 1), :],
+                w1_scales[0].bitcast(I32)[4 * q : 4 * q + 4, :].unsqueeze(0).broadcast_to([QUADRANT // 4, 4, S // 4]),
             )
 
         a_rows = [sb(f"a_rows{t}", [P, S], F32) for t in range(PACK)]
-        a_at = [sb(f"a_at{t}", [P, S], F32) for t in range(3)]
+        a_at = [sb(f"a_at{t}", [P, S], F32) for t in range(A_TILES_ON_SCALAR)]
         for t in range(PACK):
             nc.scalar.activation(a_rows[t][:], a_banks[t][:], COPY, scale=gain[:, t : t + 1])
-        for t in range(3):
+        for t in range(A_TILES_ON_SCALAR):
             for h in range(2):
                 nc.scalar.activation(a_at[t][:, half_cols(h)], a_rows[t][:].indirect(half_list(n1_t, h)), COPY)
 
-        picked_b = sb_at("picked_b", [P, 2 * S], U8, 2560)
-        nc.vector.tensor_copy(picked_b[:, S:], x_scale_tab[:].indirect(two_t[:]))
-        nc.vector.tensor_copy(picked_b[:, :S], d_scale_tab[:].indirect(k2_t[:]))
-        place_scale_rows(placed_b, picked_b)
-        x_picked_b = sb_at("x_picked_b", [P, S], U32, 512)
+        picked_b = sb_at("picked_b", [P, 2 * S], U8, AT_PICKED_B)
+        pick_scales(nc.sync, picked_b, placed_b, k2_t, two_t)
+        x_picked_b = sb_at("x_picked_b", [P, S], U32, AT_X_PICKED_B)
         nc.vector.tensor_copy(x_picked_b[:], x_tab[:].indirect(two_t[:]))
-        b_order = (0, 1, 3, 2)
-        d_picked_b = sb("d_picked_b", [P, S], U32, tag="d_words0")
-        b_banks = first_product(1, d_picked_b, k2_t, placed_b[:, :S], x_picked_b, placed_b[:, S:], b_order)
+        d_picked_b = sb("d_picked_b", [P, S], U32, tag="a_dealt_then_b_picked")
+        d_dealt_b = sb("d_dealt_b", [P, S], U32)
+        b_banks = first_product("b", PACK, d_picked_b, d_dealt_b, k2_t, x_picked_b, placed_b, (0, 1, 3, 2))
 
-        w_dealt = sb_at("w_dealt", [P, 2 * S], U8, 3072)
+        w_dealt = sb_at("w_dealt", [P, 2 * S], U8, AT_W_DEALT)
         nc.vector.tensor_copy(
             w_dealt[:].rearrange("p (t c i b) -> p c t i b", t=PACK, i=8, b=2),
             w_raw[:].rearrange("p (c i t b) -> p c t i b", t=PACK, i=8, b=2),
         )
-        w_scale_dealt = sb_at("w_scale_dealt", [P, S], U8, 2560)
+        w_scale_dealt = sb_at("w_scale_dealt", [P, S], U8, AT_W_SCALE_DEALT)
         deal_bytes(w_scale_dealt[:], w_scale_raw[:])
 
         b_rows = [sb(f"b_rows{t}", [P, S], F32) for t in range(PACK)]
-        second = sb("second", [P, PACK, S], F32)
-        for t in range(3):
-            nc.vector.scalar_tensor_tensor(second[:, t, :], b_banks[t][:], FACTOR, a_at[t][:], MULT, MULT)
-        for t in (3, 0, 1, 2):
-            nc.scalar.activation(b_rows[t][:], b_banks[t][:], COPY, scale=FACTOR)
-
+        b_at = {t: sb(f"b_at{t}", [P, S], F32) for t in range(B_TILES_ON_VECTOR, PACK)}
         first = sb("first", [P, PACK, S], F32)
-        b_at = [sb(f"b_at{t}", [P, S], F32) for t in range(PACK)]
+        second = sb("second", [P, PACK, S], F32)
         z_pairs = [sb(f"z_pairs{h}", [P, 2, HALF, 2], BF16) for h in range(2)]
         z_grouped = [sb(f"z_grouped{h}", [P, HALF * PACK], BF16) for h in range(2)]
-        z_codes = [sb(f"z_codes{h}", [P, HALF], U32) for h in range(2)]
-        z_scales = [sb(f"z_scales{h}", [P, HALF], U8) for h in range(2)]
 
-        def fetch_b(t, h):
-            nc.scalar.activation(b_at[t][:, half_cols(h)], b_rows[t][:].indirect(half_list(n2_t, h)), COPY)
+        for t in range(A_TILES_ON_SCALAR):
+            nc.vector.scalar_tensor_tensor(second[:, t, :], b_banks[t][:], FACTOR, a_at[t][:], MULT, MULT)
+        for t in [*range(A_TILES_ON_SCALAR, PACK), *range(A_TILES_ON_SCALAR)]:
+            nc.scalar.activation(b_rows[t][:], b_banks[t][:], COPY, scale=FACTOR)
+        for t in range(A_TILES_ON_SCALAR, PACK):
+            for h in range(2):
+                nc.vector.tensor_tensor(
+                    second[:, t, half_cols(h)],
+                    a_rows[t][:].indirect(half_list(n1_t, h)),
+                    b_rows[t][:, half_cols(h)],
+                    MULT,
+                )
 
-        def first_term(t, cols):
-            nc.vector.scalar_tensor_tensor(
-                first[:, t, cols], a_banks[t][:, cols], gain[:, t : t + 1], b_at[t][:, cols], MULT, MULT
-            )
+        def fetch_b(h):
+            for t in range(B_TILES_ON_VECTOR, PACK):
+                nc.scalar.activation(b_at[t][:, half_cols(h)], b_rows[t][:].indirect(half_list(n2_t, h)), COPY)
 
-        def subtract(engine, u, h):
-            engine.tensor_tensor(
+        def first_term(t, h):
+            cols = half_cols(h)
+            if t < B_TILES_ON_VECTOR:
+                nc.vector.tensor_tensor(
+                    first[:, t, cols], b_rows[t][:].indirect(half_list(n2_t, h)), a_rows[t][:, cols], MULT
+                )
+            else:
+                nc.vector.scalar_tensor_tensor(
+                    first[:, t, cols], a_banks[t][:, cols], gain[:, t : t + 1], b_at[t][:, cols], MULT, MULT
+                )
+
+        def subtract(u, h):
+            pair = slice(2 * u, 2 * u + 2)
+            nc.vector.tensor_tensor(
                 z_pairs[h][:, u, :, :].rearrange("p (c i) e -> p c e i", i=4),
-                first[:, 2 * u : 2 * u + 2, half_cols(h)].rearrange("p e (c i) -> p c e i", i=4),
-                second[:, 2 * u : 2 * u + 2, half_cols(h)].rearrange("p e (c i) -> p c e i", i=4),
+                first[:, pair, half_cols(h)].rearrange("p e (c i) -> p c e i", i=4),
+                second[:, pair, half_cols(h)].rearrange("p e (c i) -> p c e i", i=4),
                 SUB,
             )
 
-        def second_fused(t, h):
-            nc.vector.tensor_tensor(
-                second[:, t, half_cols(h)], a_rows[t][:].indirect(half_list(n1_t, h)), b_rows[t][:, half_cols(h)], MULT
-            )
-
-        def first_fused(t, h):
-            nc.vector.tensor_tensor(
-                first[:, t, half_cols(h)], b_rows[t][:].indirect(half_list(n2_t, h)), a_rows[t][:, half_cols(h)], MULT
-            )
-
         def weave(copy, h):
+            pairs = z_pairs[h][:].rearrange("p u j e -> p (u j e)").bitcast(U32)
             copy(
                 z_grouped[h][:].bitcast(U32).rearrange("p (c i u) -> p c u i", u=2, i=4),
-                z_pairs[h][:].rearrange("p u j e -> p (u j e)").bitcast(U32).rearrange("p (u c i) -> p c u i", u=2, i=4),
+                pairs.rearrange("p (u c i) -> p c u i", u=2, i=4),
             )
 
         h_pair_banks = []
         h_psum = [[], []]
 
         def last_product(h):
-            nc.vector.quantize_mx(out=z_codes[h][:].bitcast(FP8X4), scales=z_scales[h][:], in_=z_grouped[h][:])
+            z_codes = sb(f"z_codes{h}", [P, HALF], U32)
+            z_scales = sb(f"z_scales{h}", [P, HALF], U8)
+            nc.vector.quantize_mx(out=z_codes[:].bitcast(FP8X4), scales=z_scales[:], in_=z_grouped[h][:])
             for t in range(PACK):
                 if h == 0:
                     if t % 2 == 0:
-                        h_pair_banks.append(
-                            psum.tile([P, 2, HALF], F32, name=f"h0_{t}", tag=f"bank{PACK + t // 2}")
-                        )
+                        h_pair_banks.append(psum.tile([P, 2, HALF], F32, name=f"h0_{t}", tag=f"bank{PACK + t // 2}"))
                     h_psum[h].append(h_pair_banks[t // 2][:, t % 2, :])
                 else:
                     bank = psum.tile([P, HALF], F32, name=f"h1_{t}", tag=f"bank{(PACK + 2 + t) % (2 * PACK)}")
@@ -230,33 +253,28 @@ def tile_picked_twpqcrossbdif_none_po_kernel(
                     out=h_psum[h][t],
                     lhsT=w_dealt[:, t * 2 * P : (t + 1) * 2 * P].bitcast(FP4X4),
                     lhsT_scale=w_scale_dealt[:, t * P : (t + 1) * P],
-                    rhs=z_codes[h][:].bitcast(FP8X4),
-                    rhs_scale=z_scales[h][:],
+                    rhs=z_codes[:].bitcast(FP8X4),
+                    rhs_scale=z_scales[:],
                     start=True,
                     stop=True,
                 )
 
-        second_fused(3, 0)
-        second_fused(3, 1)
-        first_fused(0, 0)
-        for t in range(1, PACK):
-            fetch_b(t, 0)
-        first_term(1, half_cols(0))
-        first_fused(0, 1)
-        subtract(nc.vector, 0, 0)
-        first_term(2, half_cols(0))
-        first_term(3, half_cols(0))
-        fetch_b(1, 1)
-        fetch_b(2, 1)
-        subtract(nc.vector, 1, 0)
-        first_term(1, half_cols(1))
-        fetch_b(3, 1)
+        first_term(0, 0)
+        fetch_b(0)
+        first_term(1, 0)
+        first_term(0, 1)
+        subtract(0, 0)
+        first_term(2, 0)
+        first_term(3, 0)
+        fetch_b(1)
+        subtract(1, 0)
+        first_term(1, 1)
         weave(nc.scalar.copy, 0)
-        first_term(2, half_cols(1))
-        subtract(nc.vector, 0, 1)
-        first_term(3, half_cols(1))
+        first_term(2, 1)
+        subtract(0, 1)
+        first_term(3, 1)
         last_product(0)
-        subtract(nc.vector, 1, 1)
+        subtract(1, 1)
         weave(nc.vector.tensor_copy, 1)
         last_product(1)
 
@@ -264,17 +282,13 @@ def tile_picked_twpqcrossbdif_none_po_kernel(
         h_at = [sb(f"h_at{h}", [P, PACK, HALF], F32) for h in range(2)]
         result = [sb(f"result{h}", [P, PACK, HALF], F32) for h in range(2)]
         grouped = [sb(f"grouped{h}", [P, HALF * PACK], BF16) for h in range(2)]
-        codes = [sb(f"codes{h}", [P, HALF], U32) for h in range(2)]
         out_scales = sb("out_scales", [P, S], U8)
         out_rows = out_0.rearrange("(p t) j -> p t j", t=PACK)
         out_words = out_1[0].rearrange("p c r -> p (c r)").bitcast(I32)
 
-        def copy_h(copy, t, h):
-            copy(h_rows[t][:, half_cols(h)], h_psum[h][t])
-
         def fetch_h(t, h):
             looked_up = h_rows[t][:].indirect(half_list(n3_t, h))
-            if (t, h) in ((2, 0), (3, 0)):
+            if h == 0 and t >= H_TILES_ON_SCALAR:
                 nc.vector.tensor_copy(h_at[h][:, t, :], looked_up)
             else:
                 nc.scalar.activation(h_at[h][:, t, :], looked_up, COPY)
@@ -283,56 +297,44 @@ def tile_picked_twpqcrossbdif_none_po_kernel(
             pair = slice(2 * u, 2 * u + 2)
             nc.sync.dma_start(out_rows[:, pair, half_cols(h)], result[h][:, pair, :])
 
-        def difference(u, h):
-            pair = slice(2 * u, 2 * u + 2)
-            nc.vector.tensor_tensor(result[h][:, pair, :], h_pair_banks[u][:], h_at[h][:, pair, :], SUB)
-            store_pair(u, h)
-
-        def difference_one(t, h):
-            nc.vector.tensor_tensor(result[h][:, t, :], h_psum[h][t], h_at[h][:, t, :], SUB)
-            if t % 2 == 1:
-                store_pair(t // 2, h)
-
-        def group_aside(h):
-            nc.gpsimd.tensor_scalar(
-                grouped[h][:].rearrange("p (j t) -> p j t", t=PACK),
-                result[h][:].rearrange("p t j -> p j t"),
-                1.0,
-                0.0,
-                MULT,
-                ADD,
-            )
-
-        def group(copy, h):
-            copy(
-                grouped[h][:].rearrange("p (c i t) -> p c t i", t=PACK, i=4),
-                result[h][:].rearrange("p t (c i) -> p c t i", i=4),
-            )
-
         def quantise(h):
-            nc.vector.quantize_mx(
-                out=codes[h][:].bitcast(FP8X4), scales=out_scales[:, half_cols(h)], in_=grouped[h][:]
-            )
-            nc.sync.dma_start(out_words[:, half_cols(h)], codes[h][:].bitcast(I32))
+            codes = sb(f"codes{h}", [P, HALF], U32)
+            nc.vector.quantize_mx(out=codes[:].bitcast(FP8X4), scales=out_scales[:, half_cols(h)], in_=grouped[h][:])
+            nc.sync.dma_start(out_words[:, half_cols(h)], codes[:].bitcast(I32))
 
         for t in range(PACK):
-            copy_h(nc.scalar.copy, t, 0)
-        copy_h(nc.scalar.copy, 0, 1)
+            nc.scalar.copy(h_rows[t][:, half_cols(0)], h_psum[0][t])
+        nc.scalar.copy(h_rows[0][:, half_cols(1)], h_psum[1][0])
         for t in range(1, PACK):
-            copy_h(nc.vector.tensor_copy, t, 1)
+            nc.vector.tensor_copy(h_rows[t][:, half_cols(1)], h_psum[1][t])
+
         for t in range(PACK):
             fetch_h(t, 0)
-        difference(0, 0)
-        difference(1, 0)
-        group_aside(0)
+        for u in range(2):
+            pair = slice(2 * u, 2 * u + 2)
+            nc.vector.tensor_tensor(result[0][:, pair, :], h_pair_banks[u][:], h_at[0][:, pair, :], SUB)
+            store_pair(u, 0)
+        nc.gpsimd.tensor_scalar(
+            grouped[0][:].rearrange("p (j t) -> p j t", t=PACK),
+            result[0][:].rearrange("p t j -> p j t"),
+            1.0,
+            0.0,
+            MULT,
+            ADD,
+        )
         for t in range(PACK):
             fetch_h(t, 1)
-            difference_one(t, 1)
+            nc.vector.tensor_tensor(result[1][:, t, :], h_psum[1][t], h_at[1][:, t, :], SUB)
+            if t % 2 == 1:
+                store_pair(t // 2, 1)
         quantise(0)
-        group(nc.vector.tensor_copy, 1)
+        nc.vector.tensor_copy(
+            grouped[1][:].rearrange("p (c i t) -> p c t i", t=PACK, i=4),
+            result[1][:].rearrange("p t (c i) -> p c t i", i=4),
+        )
         quantise(1)
-        for q in range(4):
+        for q in range(BLOCKS // 4):
             queue = nc.sync if q % 2 == 0 else nc.scalar
             queue.dma_start(
-                out_2[0].bitcast(I32)[4 * q : 4 * q + 4, :], out_scales[:].bitcast(I32)[32 * q : 32 * q + 4, :]
+                out_2[0].bitcast(I32)[4 * q : 4 * q + 4, :], out_scales[:].bitcast(I32)[quadrant_rows(q), :]
             )

from contextlib import ExitStack

import concourse.mybir as mybir

F32 = mybir.dt.float32
BF16 = mybir.dt.bfloat16
I32 = mybir.dt.int32
U32 = mybir.dt.uint32
U16 = mybir.dt.uint16
U8 = mybir.dt.uint8
FP8X4 = mybir.dt.float8_e4m3fn_x4
FP4X4 = mybir.dt.float4_e2m1fn_x4
COPY = mybir.ActivationFunctionType.Copy
MULT = mybir.AluOpType.mult
ADD = mybir.AluOpType.add
SUB = mybir.AluOpType.subtract

P = 128
PACK = 4
S = 512
TOKENS = 1024
CODEWORDS = 2048
HALF = S // 2
LIST_COLS = S // 16
BLOCKS = 16
BLOCK_PARTS = 8
QUADRANT = 32
FACTOR = 0.75 * 0.0625 * 0.0625
FLOPS = 3 * 2 * S * S * S

A_TILES_ON_SCALAR = 3
B_TILES_ON_VECTOR = 1
H_TILES_ON_SCALAR = 2

AT_X_PICKED_B = 512
AT_PICKED_A = 2048
AT_PICKED_B = 2560
AT_W_SCALE_DEALT = 2560
AT_W_DEALT = 3072
AT_D_PICKED_A = 4096
AT_W_RAW = 4096
AT_W_SCALE_RAW = 5120


def tile_picked_twpqcrossbdif_none_po_kernel(
    tc, x_words, x_scales, d_words, d_scales, gn, w1_words, w1_scales, offs, k1, two, k2, n1, n2, n3,
    out_0, out_1, out_2,
):
    nc = tc.nc
    with ExitStack() as ctx:
        keep = ctx.enter_context(tc.tile_pool(name="keep", bufs=1))
        reused = ctx.enter_context(tc.tile_pool(name="reused", bufs=1))
        psum = ctx.enter_context(tc.psum_pool(name="psum", bufs=1))

        def sb(name, shape, dtype, tag=None):
            return keep.tile(shape, dtype, name=name, tag=tag or name, align_bytes=64)

        def sb_at(name, shape, dtype, offset):
            return reused.tile(shape, dtype, name=name, align_bytes=64, offset=offset)

        def half_cols(h):
            return slice(h * HALF, (h + 1) * HALF)

        def half_list(tile, h):
            return tile[:, h * (LIST_COLS // 2) : (h + 1) * (LIST_COLS // 2)]

        def quadrant_rows(q):
            return slice(QUADRANT * q, QUADRANT * q + 4)

        def load_list(name, src):
            tile = keep.tile([P, LIST_COLS], U16, name=name)
            nc.sync.dma_start(tile[:], src)
            return tile

        def load_scale_table(name, src, width):
            tile = sb(name, [P, width], U8)
            nc.scalar.dma_start(
                tile[:].bitcast(I32),
                src[0].bitcast(I32).unsqueeze(1).broadcast_to([BLOCKS, BLOCK_PARTS, width // 4]),
            )
            return tile

        def load_word_table(name, src, width):
            tile = sb(name, [P, width], U32)
            nc.sync.dma_start(tile[:].bitcast(I32), src[0].rearrange("p c r -> p (c r)").bitcast(I32))
            return tile

        offs_t = load_list("offs_t", offs)
        x_scale_tab = load_scale_table("x_scale_tab", x_scales, TOKENS)
        k1_t = load_list("k1_t", k1)
        d_scale_tab = load_scale_table("d_scale_tab", d_scales, CODEWORDS)
        two_t = load_list("two_t", two)
        x_tab = load_word_table("x_tab", x_words, TOKENS)
        k2_t = load_list("k2_t", k2)
        d_tab = load_word_table("d_tab", d_words, CODEWORDS)
        n1_t = load_list("n1_t", n1)
        n2_t = load_list("n2_t", n2)
        n3_t = load_list("n3_t", n3)

        placed_a = sb("placed_a", [P, 2 * S], U8)
        placed_b = sb("placed_b", [P, 2 * S], U8)
        for tile in (placed_a, placed_b):
            nc.vector.memset(tile[:].bitcast(I32), 0)
        gain = sb("gain", [P, PACK], F32)
        nc.gpsimd.dma_start(gain[:], gn.rearrange("(p t) o -> p (t o)", t=PACK))

        def pick_scales(queue, picked, placed, d_list, x_list):
            nc.vector.tensor_copy(picked[:, S:], x_scale_tab[:].indirect(x_list[:]))
            nc.vector.tensor_copy(picked[:, :S], d_scale_tab[:].indirect(d_list[:]))
            for q in range(BLOCKS // 4):
                queue.dma_start(
                    placed[:].bitcast(I32)[quadrant_rows(q), :],
                    picked[:].bitcast(I32)[QUADRANT * q : QUADRANT * (q + 1) : BLOCK_PARTS, :],
                )

        def deal_bytes(dealt, plain):
            nc.vector.tensor_copy(
                dealt.rearrange("p (t c i) -> p c t i", t=PACK, i=16),
                plain.rearrange("p (c i t) -> p c t i", t=PACK, i=16),
            )

        def first_product(name, first_bank, d_picked, d_dealt, d_list, x_picked, placed, order):
            nc.vector.tensor_copy(d_picked[:], d_tab[:].indirect(d_list[:]))
            nc.vector.tensor_copy(
                d_dealt[:].rearrange("p (t c i) -> p c t i", t=PACK, i=4),
                d_picked[:].rearrange("p (c i t) -> p c t i", t=PACK, i=4),
            )
            d_scale_dealt = sb(f"d_scale_dealt_{name}", [P, S], U8)
            deal_bytes(d_scale_dealt[:], placed[:, :S])
            banks = {}
            for t in order:
                banks[t] = psum.tile([P, S], F32, name=f"{name}{t}", tag=f"bank{first_bank + t}")
                cols = slice(t * P, (t + 1) * P)
                nc.tensor.matmul_mx(
                    out=banks[t][:],
                    lhsT=d_dealt[:, cols].bitcast(FP8X4),
                    lhsT_scale=d_scale_dealt[:, cols],
                    rhs=x_picked[:].bitcast(FP8X4),
                    rhs_scale=placed[:, S:],
                    start=True,
                    stop=True,
                )
            return banks

        picked_a = sb_at("picked_a", [P, 2 * S], U8, AT_PICKED_A)
        pick_scales(nc.scalar, picked_a, placed_a, k1_t, offs_t)
        x_picked_a = sb("x_picked_a", [P, S], U32)
        nc.vector.tensor_copy(x_picked_a[:], x_tab[:].indirect(offs_t[:]))
        d_picked_a = sb_at("d_picked_a", [P, S], U32, AT_D_PICKED_A)
        d_dealt_a = sb("d_dealt_a", [P, S], U32, tag="a_dealt_then_b_picked")
        a_banks = first_product("a", 0, d_picked_a, d_dealt_a, k1_t, x_picked_a, placed_a, range(PACK))

        w_raw = sb_at("w_raw", [P, 2 * S], U8, AT_W_RAW)
        nc.sync.dma_start(w_raw[:].bitcast(I32), w1_words[0].bitcast(I32))
        w_scale_raw = sb_at("w_scale_raw", [P, S], U8, AT_W_SCALE_RAW)
        for q in range(BLOCKS // 4):
            nc.sync.dma_start(
                w_scale_raw[:].bitcast(I32)[QUADRANT * q : QUADRANT * (q + 1), :],
                w1_scales[0].bitcast(I32)[4 * q : 4 * q + 4, :].unsqueeze(0).broadcast_to([QUADRANT // 4, 4, S // 4]),
            )

        a_rows = [sb(f"a_rows{t}", [P, S], F32) for t in range(PACK)]
        a_at = [sb(f"a_at{t}", [P, S], F32) for t in range(A_TILES_ON_SCALAR)]
        for t in range(PACK):
            nc.scalar.activation(a_rows[t][:], a_banks[t][:], COPY, scale=gain[:, t : t + 1])
        for t in range(A_TILES_ON_SCALAR):
            for h in range(2):
                nc.scalar.activation(a_at[t][:, half_cols(h)], a_rows[t][:].indirect(half_list(n1_t, h)), COPY)

        picked_b = sb_at("picked_b", [P, 2 * S], U8, AT_PICKED_B)
        pick_scales(nc.sync, picked_b, placed_b, k2_t, two_t)
        x_picked_b = sb_at("x_picked_b", [P, S], U32, AT_X_PICKED_B)
        nc.vector.tensor_copy(x_picked_b[:], x_tab[:].indirect(two_t[:]))
        d_picked_b = sb("d_picked_b", [P, S], U32, tag="a_dealt_then_b_picked")
        d_dealt_b = sb("d_dealt_b", [P, S], U32)
        b_banks = first_product("b", PACK, d_picked_b, d_dealt_b, k2_t, x_picked_b, placed_b, (0, 1, 3, 2))

        w_dealt = sb_at("w_dealt", [P, 2 * S], U8, AT_W_DEALT)
        nc.vector.tensor_copy(
            w_dealt[:].rearrange("p (t c i b) -> p c t i b", t=PACK, i=8, b=2),
            w_raw[:].rearrange("p (c i t b) -> p c t i b", t=PACK, i=8, b=2),
        )
        w_scale_dealt = sb_at("w_scale_dealt", [P, S], U8, AT_W_SCALE_DEALT)
        deal_bytes(w_scale_dealt[:], w_scale_raw[:])

        b_rows = [sb(f"b_rows{t}", [P, S], F32) for t in range(PACK)]
        b_at = {t: sb(f"b_at{t}", [P, S], F32) for t in range(B_TILES_ON_VECTOR, PACK)}
        first = sb("first", [P, PACK, S], F32)
        second = sb("second", [P, PACK, S], F32)
        z_pairs = [sb(f"z_pairs{h}", [P, 2, HALF, 2], BF16) for h in range(2)]
        z_grouped = [sb(f"z_grouped{h}", [P, HALF * PACK], BF16) for h in range(2)]

        for t in range(A_TILES_ON_SCALAR):
            nc.vector.scalar_tensor_tensor(second[:, t, :], b_banks[t][:], FACTOR, a_at[t][:], MULT, MULT)
        for t in [*range(A_TILES_ON_SCALAR, PACK), *range(A_TILES_ON_SCALAR)]:
            nc.scalar.activation(b_rows[t][:], b_banks[t][:], COPY, scale=FACTOR)
        for t in range(A_TILES_ON_SCALAR, PACK):
            for h in range(2):
                nc.vector.tensor_tensor(
                    second[:, t, half_cols(h)],
                    a_rows[t][:].indirect(half_list(n1_t, h)),
                    b_rows[t][:, half_cols(h)],
                    MULT,
                )

        def fetch_b(h):
            for t in range(B_TILES_ON_VECTOR, PACK):
                nc.scalar.activation(b_at[t][:, half_cols(h)], b_rows[t][:].indirect(half_list(n2_t, h)), COPY)

        def first_term(t, h):
            cols = half_cols(h)
            if t < B_TILES_ON_VECTOR:
                nc.vector.tensor_tensor(
                    first[:, t, cols], b_rows[t][:].indirect(half_list(n2_t, h)), a_rows[t][:, cols], MULT
                )
            else:
                nc.vector.scalar_tensor_tensor(
                    first[:, t, cols], a_banks[t][:, cols], gain[:, t : t + 1], b_at[t][:, cols], MULT, MULT
                )

        def subtract(u, h):
            pair = slice(2 * u, 2 * u + 2)
            nc.vector.tensor_tensor(
                z_pairs[h][:, u, :, :].rearrange("p (c i) e -> p c e i", i=4),
                first[:, pair, half_cols(h)].rearrange("p e (c i) -> p c e i", i=4),
                second[:, pair, half_cols(h)].rearrange("p e (c i) -> p c e i", i=4),
                SUB,
            )

        def weave(copy, h):
            pairs = z_pairs[h][:].rearrange("p u j e -> p (u j e)").bitcast(U32)
            copy(
                z_grouped[h][:].bitcast(U32).rearrange("p (c i u) -> p c u i", u=2, i=4),
                pairs.rearrange("p (u c i) -> p c u i", u=2, i=4),
            )

        h_pair_banks = []
        h_psum = [[], []]

        def last_product(h):
            z_codes = sb(f"z_codes{h}", [P, HALF], U32)
            z_scales = sb(f"z_scales{h}", [P, HALF], U8)
            nc.vector.quantize_mx(out=z_codes[:].bitcast(FP8X4), scales=z_scales[:], in_=z_grouped[h][:])
            for t in range(PACK):
                if h == 0:
                    if t % 2 == 0:
                        h_pair_banks.append(psum.tile([P, 2, HALF], F32, name=f"h0_{t}", tag=f"bank{PACK + t // 2}"))
                    h_psum[h].append(h_pair_banks[t // 2][:, t % 2, :])
                else:
                    bank = psum.tile([P, HALF], F32, name=f"h1_{t}", tag=f"bank{(PACK + 2 + t) % (2 * PACK)}")
                    h_psum[h].append(bank[:])
                nc.tensor.matmul_mx(
                    out=h_psum[h][t],
                    lhsT=w_dealt[:, t * 2 * P : (t + 1) * 2 * P].bitcast(FP4X4),
                    lhsT_scale=w_scale_dealt[:, t * P : (t + 1) * P],
                    rhs=z_codes[:].bitcast(FP8X4),
                    rhs_scale=z_scales[:],
                    start=True,
                    stop=True,
                )

        first_term(0, 0)
        fetch_b(0)
        first_term(1, 0)
        first_term(0, 1)
        subtract(0, 0)
        first_term(2, 0)
        first_term(3, 0)
        fetch_b(1)
        subtract(1, 0)
        first_term(1, 1)
        weave(nc.scalar.copy, 0)
        first_term(2, 1)
        subtract(0, 1)
        first_term(3, 1)
        last_product(0)
        subtract(1, 1)
        weave(nc.vector.tensor_copy, 1)
        last_product(1)

        h_rows = [sb(f"h_rows{t}", [P, S], F32) for t in range(PACK)]
        h_at = [sb(f"h_at{h}", [P, PACK, HALF], F32) for h in range(2)]
        result = [sb(f"result{h}", [P, PACK, HALF], F32) for h in range(2)]
        grouped = [sb(f"grouped{h}", [P, HALF * PACK], BF16) for h in range(2)]
        out_scales = sb("out_scales", [P, S], U8)
        out_rows = out_0.rearrange("(p t) j -> p t j", t=PACK)
        out_words = out_1[0].rearrange("p c r -> p (c r)").bitcast(I32)

        def fetch_h(t, h):
            looked_up = h_rows[t][:].indirect(half_list(n3_t, h))
            if h == 0 and t >= H_TILES_ON_SCALAR:
                nc.vector.tensor_copy(h_at[h][:, t, :], looked_up)
            else:
                nc.scalar.activation(h_at[h][:, t, :], looked_up, COPY)

        def store_pair(u, h):
            pair = slice(2 * u, 2 * u + 2)
            nc.sync.dma_start(out_rows[:, pair, half_cols(h)], result[h][:, pair, :])

        def quantise(h):
            codes = sb(f"codes{h}", [P, HALF], U32)
            nc.vector.quantize_mx(out=codes[:].bitcast(FP8X4), scales=out_scales[:, half_cols(h)], in_=grouped[h][:])
            nc.sync.dma_start(out_words[:, half_cols(h)], codes[:].bitcast(I32))

        for t in range(PACK):
            nc.scalar.copy(h_rows[t][:, half_cols(0)], h_psum[0][t])
        nc.scalar.copy(h_rows[0][:, half_cols(1)], h_psum[1][0])
        for t in range(1, PACK):
            nc.vector.tensor_copy(h_rows[t][:, half_cols(1)], h_psum[1][t])

        for t in range(PACK):
            fetch_h(t, 0)
        for u in range(2):
            pair = slice(2 * u, 2 * u + 2)
            nc.vector.tensor_tensor(result[0][:, pair, :], h_pair_banks[u][:], h_at[0][:, pair, :], SUB)
            store_pair(u, 0)
        nc.gpsimd.tensor_scalar(
            grouped[0][:].rearrange("p (j t) -> p j t", t=PACK),
            result[0][:].rearrange("p t j -> p j t"),
            1.0,
            0.0,
            MULT,
            ADD,
        )
        for t in range(PACK):
            fetch_h(t, 1)
            nc.vector.tensor_tensor(result[1][:, t, :], h_psum[1][t], h_at[1][:, t, :], SUB)
            if t % 2 == 1:
                store_pair(t // 2, 1)
        quantise(0)
        nc.vector.tensor_copy(
            grouped[1][:].rearrange("p (c i t) -> p c t i", t=PACK, i=4),
            result[1][:].rearrange("p t (c i) -> p c t i", i=4),
        )
        quantise(1)
        for q in range(BLOCKS // 4):
            queue = nc.sync if q % 2 == 0 else nc.scalar
            queue.dma_start(
                out_2[0].bitcast(I32)[4 * q : 4 * q + 4, :], out_scales[:].bitcast(I32)[quadrant_rows(q), :]
            )
